import numpy as np, ml_dtypes
CORES = [3,7,11,15,131,135,139,143]
N = 8
import mx_ref
BF = ml_dtypes.bfloat16
def entries(a):
    return np.ascontiguousarray(a.T).reshape(-1)
def table(e):
    return np.ascontiguousarray(np.reshape(e, (-1, 16)).T).astype(np.int32)
def pick(q, e):
    c = np.concatenate([q[0].reshape(128, -1, 4), np.zeros((128, 1, 4), np.uint8)], axis=1); s = np.concatenate([q[1], np.ones((16, 1), np.uint8)], axis=1)
    return (np.ascontiguousarray(c[:, e].reshape(128, -1)), np.ascontiguousarray(s[:, e]))
def join(*qs):
    return (np.concatenate([q[0] for q in qs], axis=1), np.concatenate([q[1] for q in qs], axis=1))
def put(q, e, v):
    c, s = q[0].reshape(128, -1, 4).copy(), q[1].copy(); c[:, e] = v[0].reshape(128, -1, 4); s[:, e] = v[1]
    return (c.reshape(128, -1), s)
def pk(c, s):
    return (np.ascontiguousarray(c), mx_ref.live(s))
def emit(q):
    return q[0], q[1]
def decode(q):
    o = []
    for b in range(4):
        e = np.zeros((128, 128, 4), np.float32); e[np.arange(128), np.arange(128), b] = 1
        o.append(mx_ref.matmul(mx_ref.quantize(e.reshape(128, 512).astype(BF)), q))
    return np.stack(o, axis=2).reshape(128, -1)
def cut(t, i, w=512):
    return t[:, w * i:w * i + w]
def f(rng, *shape):
    return mx_ref.flush((rng.standard_normal(shape, dtype=np.float32) * np.exp2(rng.integers(-2, 3, shape[:-1] + (1,)))).astype(BF))
def wide(rng, *shape, cols=0):
    v = rng.standard_normal(shape, dtype=np.float32) * np.exp2(rng.integers(-12, 13, shape)).astype(np.float32)
    if cols: v *= np.repeat(np.exp2(rng.integers(-cols, cols + 1, shape[:-2] + (1, shape[-1] // 4))) * (rng.random(shape[:-2] + (1, shape[-1] // 4)) > 0.0625), 4, axis=-1).astype(np.float32)
    return mx_ref.flush(v.astype(BF))
P, M, A, CAPP, R = 256, 64, 32, 16, 2
def big(v):
    v = v.astype(np.float32)
    v[np.abs(v) < np.float32(2.0 ** -16)] = 0
    return v.astype(BF)
def listed(e):
    return np.stack([table(v) for v in e])
def setup_inputs(rng):
    return {"ky": big(f(rng, N, 128, 4 * P)), "nx": listed(rng.integers(0, N * M, (N, P))), "x": big(f(rng, N, 128, 4 * A)), "st": listed(rng.integers(0, N * M, (N, A))), "w": f(rng, N, 128, 512)}
def setup_inputs_spread(rng):
    d = setup_inputs(rng)
    d["ky"] = big(wide(rng, N, 128, 4 * P, cols=6))
    d["x"] = big(wide(rng, N, 128, 4 * A, cols=4))
    return d
def setup_inputs_ties(rng):
    d = setup_inputs(rng)
    o = np.argsort(rng.random((N, M, 4)), axis=2) % 2
    v = d["ky"].reshape(N, 128, M, 4, 4)
    v = np.ascontiguousarray(np.stack([np.take_along_axis(v[r], np.broadcast_to(o[r][None, :, :, None], (128, M, 4, 4)), axis=2) for r in range(N)]))
    for r in range(N): v[r][:, rng.permutation(M)[:M // 8]] = 0
    d["ky"] = v.reshape(N, 128, 4 * P)
    to = np.argsort(rng.random((N, M, N)), axis=2)[:, :, :4]
    d["nx"] = listed((to * M + rng.integers(0, M, (N, M, 4))).reshape(N, P))
    return d
def setup_inputs_crowd(rng):
    d = setup_inputs(rng)
    o, st = rng.permutation(N), np.zeros((N, A), int)
    for i in range(N):
        s, to = o[i], o[(i + 1) % N]
        here = rng.permutation(A) < (CAPP if i % 2 == 0 else A - CAPP // 4)
        near = to * M + (rng.integers(0, M, A) if i % 2 == 0 else np.full(A, int(rng.integers(0, M))))
        far = (to + rng.integers(1, N, A)) % N * M + rng.integers(0, M, A)
        st[s] = np.where(here, near, far)
    d["st"] = listed(st)
    return d
def kept(rng, *shape):
    return 4 * rng.integers(0, M // 4, shape) + rng.integers(0, 3, shape)
def setup_inputs_stay(rng):
    d = setup_inputs(rng)
    o = rng.permutation(N)
    z, z2 = int(o[0]), int(o[1])
    v = np.arange(M)[None, :, None]
    to = np.arange(N)[:, None, None] * M + np.where(v % 2 == 0, v, kept(rng, N, M, 4))
    to[z, 3::4] = o[rng.integers(2, N, (M // 4, 4))] * M + rng.integers(0, M, (M // 4, 4))
    to[z2] = z * M + kept(rng, M, 4)
    d["nx"] = listed(to.reshape(N, P))
    leave = np.zeros((N, A), bool)
    leave[:, :CAPP] = np.argsort(rng.random((N, CAPP)), axis=1) < CAPP // 4
    st = z * M + np.where(leave, 4 * rng.integers(0, M // 4, (N, A)) + 3, kept(rng, N, A))
    n = CAPP + CAPP // 2
    st[:, n:] = z2 * M + rng.integers(0, M, (N, A - n))
    low = rng.permutation(N) < N // 2
    st[low] = np.roll(st[low], A - n, axis=1)
    d["st"] = listed(st)
    return d
def setup_inputs_turn(rng):
    d = setup_inputs(rng)
    sign = rng.choice([-1.0, 1.0], (128, 4))
    top = np.arange(128) < 64
    o = np.argsort(rng.random((N, M, 4)), axis=2).reshape(N, P)
    g = np.where(top[None, :, None], np.exp2(-2.0 * o)[:, None, :], np.exp2(2.0 * o + 2)[:, None, :])
    d["ky"] = big(((1 + rng.random((N, 128, P, 4))) * g[..., None] * sign[None, :, None, :]).reshape(N, 128, 4 * P))
    d["x"] = big(((1 + rng.random((N, 128, A, 4))) * top[None, :, None, None] * sign[None, :, None, :]).reshape(N, 128, 4 * A))
    return d
def check_inputs(d):
    b = []
    for k, lo, hi in (("ky", -16, 24), ("x", -16, 24), ("w", -30, 30)):
        v = np.abs(d[k].astype(np.float32))
        if not (np.isfinite(v).all() and ((v == 0) | (v >= 2.0 ** lo) & (v <= 2.0 ** hi)).all()): b.append("a value of " + k)
    for k in ("nx", "st"):
        if d[k].min() < 0 or d[k].max() >= N * M: b.append("an entry of " + k)
    return b
def served(node):
    ok = np.zeros(N * A, bool)
    for s in range(N):
        at = node[A * s:A * s + A] // M
        for d in range(N): ok[A * s + np.flatnonzero(at == d)[:CAPP]] = True
    return np.flatnonzero(ok)
def reference(ky, nx, x, st, w):
    pieces = [mx_ref.quantize(np.ascontiguousarray(cut(ky[d], i))) for d in range(N) for i in range(P // 128)]
    dk = decode(join(*pieces)).reshape(128, N * P, 4)
    leads = np.concatenate([entries(nx[d]) for d in range(N)])
    q = join(*[mx_ref.quantize(np.ascontiguousarray(x[s])) for s in range(N)])
    node = np.concatenate([entries(st[s]) for s in range(N)])
    e = np.arange(N * A)
    way = [node]
    for t in range(R):
        go = served(node)
        z = np.concatenate([mx_ref.matmul(p, q) for p in pieces])
        four = 4 * node[:, None] + np.arange(4)
        k = 4 * node + np.argmax(z[four, e[:, None]] + np.float32(0), axis=1)
        v = decode(q).reshape(128, N * A, 4) * np.float32(0.5) + dk[:, k] * np.float32(0.5)
        new = mx_ref.quantize(np.ascontiguousarray(v.reshape(128, -1).astype(BF)))
        q = put(q, go, pick(new, go))
        node = node.copy()
        node[go] = leads[k[go]]
        way.append(node)
    oc, osc = np.zeros((N, 128, 4 * A), np.uint8), np.zeros((N, 16, A), np.uint8)
    nd, y = np.zeros((N, R + 1, A), np.float32), np.zeros((N, 128, A), np.float32)
    for s in range(N):
        own = pick(q, np.arange(A * s, A * s + A))
        oc[s], osc[s] = emit(own)
        nd[s] = np.stack(way)[:, A * s:A * s + A]
        y[s] = mx_ref.matmul(mx_ref.quantize(np.ascontiguousarray(w[s])), own)
    return {"oc": oc, "osc": osc, "nd": nd, "y": y}

@@ -1,0 +1,447 @@
+from concourse.bass import DstId, RemoteDMATransfer
+from concourse.mybir import dt, AluOpType, AxisListType, ActivationFunctionType
+
+N, P, A, CAPP = 8, 256, 32, 16
+F8, U8, F32, BF, I32, U16 = "float8_e4m3fn_x4", "uint8", "float32", "bfloat16", "int32", "uint16"
+
+SCRATCH = {}
+
+
+def _add(name, cols, dtype, where="sbuf"):
+    SCRATCH[name] = (where, [128, cols], dtype)
+
+
+def _pair(name, cols):
+    _add(name + "c", cols, F8)
+    _add(name + "s", cols, U8)
+
+
+for _n, _c in (("qx", 128), ("lx0", 256), ("send0", 32), ("land0", 128), ("new0", 128), ("wina", 256), ("send1", 128),
+               ("land1", 128), ("new1", 128), ("winb", 160), ("fin", 128), ("kq", 256), ("wq", 128), ("h", 512)):
+    _pair(_n, _c)
+for _n, _c, _d in (("xt", 512, BF), ("kt", 1024, BF), ("wt", 512, BF), ("hr", 516, BF), ("hb", 516, BF), ("hk", 1024, BF),
+                   ("iop", 64, I32), ("ioj", 64, I32), ("p15", 64, I32), ("pd", 64, I32), ("j15", 64, I32), ("mm", 64, F32),
+                   ("dm", 64, F32), ("blk", 8, F32), ("pdf", 1, F32), ("r1", 1, F32), ("ibq", 4, F32), ("af", 32, F32),
+                   ("pi", 16, U16), ("rst", 256, F32), ("fs", 8, F32), ("cc", 8, F32), ("one", 32, F32),
+                   ("str1", 32, I32), ("strb", 32, I32), ("nx1", 256, I32), ("nxr", 256, I32), ("nxf", 256, F32),
+                   ("lsh", 8, I32), ("lsa", 8, F32), ("lsu", 8, U16),
+                   ("pl", 2, U16), ("sl", 8, U16), ("nr2", 32, F32), ("ys", 32, F32),
+                   ("vv", 32, I32), ("xx", 33, F32), ("dx", 32, F32), ("eq", 32, F32), ("cum", 32, F32), ("lt", 32, F32),
+                   ("pr", 33, F32), ("xs", 1, F32), ("vi", 8, I32), ("vm", 8, F32), ("v", 1, F32), ("zlf", 4, F32),
+                   ("ng", 64, F32), ("n4", 4, F32), ("dn", 3, F32), ("zs", 256, F32), ("zg", 64, F32), ("rm", 64, F32),
+                   ("ll", 4, F32), ("c", 1, F32), ("npr", 4, F32), ("ct", 8, U16), ("dq", 512, F32),
+                   ("e8", 256, F32), ("c8", 256, F32), ("rk", 32, F32), ("sv", 32, F32), ("ta", 32, F32), ("tb", 32, F32),
+                   ("l2", 2, F32), ("na", 32, F32), ("nb", 32, F32), ("n2", 2, F32), ("e", 32, F32), ("et", 32, F32), ("u", 4, F32)):
+    _add(_n, _c, _d)
+for _t in ("0", "1"):
+    for _n, _c, _d in (("nri", 32, I32), ("dr", 32, I32), ("loc64", 32, F32), ("ti", 8, I32), ("shx", 8, I32), ("xr", 32, I32),
+                       ("zl", 4, U16), ("node", 1, F32), ("nt", 512, BF), ("rn", 8, F32), ("row", 128, F32), ("mrs", 160, F32),
+                       ("lu", 2, U16), ("nu", 2, U16)):
+        _add(_n + _t, _c, _d)
+_add("bank", 512 * 6, F32, "psum")
+
+ARRIVE = ["lx0", "xr0", "rn0", "ret0", "xr1", "land1", "rn1", "ret1"]
+DMAS = ["st", "x", "ky", "nx", "w", "own0", "nd0", "rnown0", "rnown1", "row0", "row1", "self0", "self1", "own1", "nd1", "nd2", "oc", "osc", "y"]
+SEMAPHORES = ["sg", "sv", "sa", "sp", "left"] + ["a_" + k for k in ARRIVE] + ["d_" + k for k in DMAS]
+
+
+def _bits(m):
+    return bin(m).count("1")
+
+
+def _plan(topo, cores, me):
+    others = [c for c in cores if c != me]
+    near = [c for c in others if c in topo.cores_of(me)]
+    far = [c for c in others if c not in near]
+    mate = [c for c in far if topo.mates(me, c) and topo.die(me) == topo.die(c)]
+    port = topo.engines(me, far[0])
+    rest = [e for e in topo.engines(me, near[0]) if e not in port]
+    load = {e: 0 for e in port}
+    turn = [0]
+
+    def masks(dsts):
+        o = {}
+        for c in dsts:
+            if c in near:
+                o[c] = sum(1 << e for e in rest)
+        f = [c for c in dsts if c in far]
+        if len(f) == 1:
+            o[f[0]] = sum(1 << e for e in port)
+            return o
+        k = turn[0] % len(f)
+        turn[0] += 2
+        f = f[k:] + f[:k]
+        free = sorted(port, key=lambda e: load[e])
+        doubles = len(free) - len(f)
+        for i, c in enumerate(f):
+            take = 1 if i < len(f) - doubles else 2
+            o[c] = sum(1 << e for e in free[:take])
+            for e in free[:take]:
+                load[e] += 2 // take
+            free = free[take:]
+        return o
+
+    picked = near + mate
+    wide = [c for c in far if c not in picked]
+    out = {"wide_c": masks(wide), "wide_s": masks(wide), "xr0": masks(others), "pick_c": masks(picked), "pick_s": masks(picked)}
+    for k in ("rn0", "ret0_c", "ret0_s", "xr1", "land1_c", "land1_s", "rn1", "ret1_c", "ret1_s"):
+        out[k] = masks(others)
+    return out, picked, wide
+
+
+ROUTE = {"wide_c": "lx0", "wide_s": "lx0", "pick_c": "lx0", "pick_s": "lx0", "xr0": "xr0", "rn0": "rn0", "ret0_c": "ret0", "ret0_s": "ret0",
+         "xr1": "xr1", "land1_c": "land1", "land1_s": "land1", "rn1": "rn1", "ret1_c": "ret1", "ret1_s": "ret1"}
+
+
+def rank_program(g, core, T, topo):
+    rank = T.rank_of(core)
+    if rank is None:
+        return
+    cores = list(T.cores)
+    others = [c for c in cores if c != core]
+    plans = {c: _plan(topo, cores, c) for c in cores}
+    calls, picked, wide = plans[core]
+    want = {k: 0 for k in ARRIVE}
+    for c in others:
+        for k, a in ROUTE.items():
+            want[a] += _bits(plans[c][0][k].get(core, 0))
+    ALU, X, CP = AluOpType, AxisListType.X, ActivationFunctionType.Copy
+    queues = {"g": g, "v": g.vector, "a": g.scalar, "p": g.tensor, "s": g.sync}
+    sems = {"g": "sg", "v": "sv", "a": "sa", "p": "sp"}
+    count = {k: 0 for k in sems}
+    known = {k: {} for k in queues}
+    snap = {}
+    wrote, readers = {}, {}
+
+    def waits(q, reads, writes):
+        need = [wrote[k] for k in reads]
+        for k in writes:
+            if k in wrote:
+                need.append(wrote[k])
+            for e, rq in readers.get(k, []):
+                if rq != q or e[0].startswith("d_"):
+                    need.append(e)
+        best = {}
+        for s, val in need:
+            if known[q].get(s, 0) < val:
+                best[s] = max(best.get(s, 0), val)
+        for s in sorted(best, key=lambda s: -len(snap.get((s, best[s]), {}))):
+            val = best[s]
+            if known[q].get(s, 0) >= val:
+                continue
+            queues[q].wait_ge(T.sem[s], val)
+            known[q][s] = val
+            for s2, v2 in snap.get((s, val), {}).items():
+                known[q][s2] = max(known[q].get(s2, 0), v2)
+
+    def note(q, ev, reads, writes):
+        snap[ev] = dict(known[q])
+        for k in reads:
+            readers.setdefault(k, []).append((ev, q))
+        for k in writes:
+            wrote[k] = ev
+            readers[k] = []
+
+    def op(q, fn, reads, writes):
+        waits(q, reads, writes)
+        count[q] += 1
+        fn(queues[q]).then_inc(T.sem[sems[q]], 1)
+        note(q, (sems[q], count[q]), reads, writes)
+
+    dcount = {}
+
+    def dma(q, name, out, in_, reads, writes):
+        s = "d_" + name
+        waits(q, reads, writes)
+        queues[q].dma_start(out, in_).then_inc(T.sem[s], 16)
+        dcount[s] = dcount.get(s, 0) + 16
+        note(q, (s, dcount[s]), reads, writes)
+
+    left = [0]
+
+    def send(call, src, dst, reads):
+        waits("g", reads, [])
+        tr = []
+        for c, m in calls[call].items():
+            rid, pid = topo.addr(c, core)
+            tr.append(RemoteDMATransfer(dst_ids=[DstId(rid=rid, pnc=pid)], dma_engine_mask=m, remote_sem=T.sem["a_" + ROUTE[call]],
+                                        src=src(cores.index(c)), dst=dst(cores.index(c))))
+            left[0] += _bits(m)
+        g.remote_dma_fused(tr, local_sem=T.sem.left)
+
+    for k in ARRIVE:
+        wrote["in_" + k] = ("a_" + k, want[k])
+
+    def codes(name, a, b):
+        return T[name + "c"][:, a:b].bitcast(dt.uint8)
+
+    def words(name, a, b):
+        return T[name + "c"][:, a:b].bitcast(dt.uint32)
+
+    def ts(out, in0, s1, op0, reads, writes, s2=None, op1=None):
+        if op1 is None:
+            op("v", lambda e: e.tensor_scalar(out, in0, s1, None, op0), reads, writes)
+        else:
+            op("v", lambda e: e.tensor_scalar(out, in0, s1, s2, op0, op1), reads, writes)
+
+    def tt(out, a, b, o, reads, writes):
+        op("v", lambda e: e.tensor_tensor(out, a, b, o), reads, writes)
+
+    def cp(out, a, reads, writes):
+        op("v", lambda e: e.tensor_copy(out, a), reads, writes)
+
+    def red(out, a, reads, writes, o=ALU.add):
+        op("v", lambda e: e.tensor_reduce(out, a, X, o), reads, writes)
+
+    def fill(ap, value, writes):
+        op("v", lambda e: e.memset(ap, value), [], writes)
+
+    def quant(name, a, b, tile, reads, writes):
+        op("v", lambda e: e.quantize_mx(T[name + "c"][:, a:b], T[name + "s"][:, a:b], tile), reads, writes)
+
+    def mx(bank, n, l, la, r, ra, reads):
+        op("p", lambda e: e.matmul_mx(T.bank[:, 512 * bank:512 * bank + n], T[l + "c"][:, la:la + 128], T[l + "s"][:, la:la + 128],
+                                      T[r + "c"][:, ra:ra + n], T[r + "s"][:, ra:ra + n], True, True), reads, ["bank%d" % bank])
+
+    def bank(k, n):
+        return T.bank[:, 512 * k:512 * k + n]
+
+    def act(out, in_, reads, writes):
+        op("a", lambda e: e.activation(out, in_, CP), reads, writes)
+
+    def pick(out, oa, win, wb, off, n, reads, key):
+        cp(words(out, oa, oa + n), words(win, 0, wb).indirect(off), reads, [key + "_c"])
+        act(T[out + "s"][:, oa:oa + n], T[win + "s"][:, 0:wb].indirect(off), reads, [key + "_s"])
+
+    dma("s", "st", T.str1[0:1, 0:A], T.st[:], [], ["str1"])
+    dma("a", "x", T.xt[:, 0:4 * A], T.x[:], [], ["xt"])
+    dma("s", "ky", T.kt[:], T.ky[:], [], ["kt"])
+    dma("a", "nx", T.nx1[0:1, 0:P], T.nx[:], [], ["nx1"])
+    op("g", lambda e: e.iota(T.iop[:], [[0, 64]], 0, 1), [], ["iop"])
+    op("g", lambda e: e.iota(T.ioj[:], [[1, 64]], 0, 0), [], ["ioj"])
+    fill(T.hr[:], 0.5, ["hr"])
+    fill(T.xt[:, 4 * A:512], 0.0, ["xtz"])
+    op("g", lambda e: e.affine_select(T.hb[:], T.hr[:], [[-1, 516]], ALU.is_equal, 0.0, 3, 4), ["hr"], ["hb"])
+    ts(T.p15[:], T.iop[:], 15, ALU.bitwise_and, ["iop"], ["p15"])
+    ts(T.pd[:], T.iop[:], 4, ALU.arith_shift_right, ["iop"], ["pd"])
+    ts(T.j15[:], T.ioj[:], 15, ALU.bitwise_and, ["ioj"], ["j15"])
+    fill(T.one[:], 1.0, ["one"])
+    cp(T.pdf[:], T.pd[:, 0:1], ["pd"], ["pdf"])
+    ts(T.r1[:], T.p15[:, 0:1], 1.0, ALU.add, ["p15"], ["r1"])
+    tt(T.mm[:], T.p15[:], T.j15[:], ALU.is_equal, ["p15", "j15"], ["mm"])
+    ts(T.loc640[:], T.ioj[:, 0:A], 64.0, ALU.mult, ["ioj"], ["loc640"])
+    fill(T.xx[:, A:A + 1], 0.0, ["xxz"])
+    tt(T.blk[:], T.pd[:, 0:N], T.ioj[:, 0:N], ALU.is_equal, ["pd", "ioj"], ["blk"])
+    ts(T.ibq[:], T.ioj[:, 0:4], 0.25, ALU.mult, ["ioj"], ["ibq"])
+    ts(T.dm[:], T.mm[:], -1.0, ALU.add, ["mm"], ["dm"], 1e29, ALU.mult)
+    fill(T.fs[:], 1.0, ["fs"])
+    ts(T.cc[:], T.ioj[:, 0:N], 32.0, ALU.mult, ["ioj"], ["cc"])
+    for s, c in enumerate(cores):
+        if c != core and core in plans[c][1]:
+            fill(T.fs[:, s:s + 1], 0.0, ["fs"])
+            ts(T.cc[:, s:s + 1], T.p15[:, 0:1], float(32 * s), ALU.add, ["p15"], ["cc"])
+
+    quant("qx", 0, 128, T.xt[:], ["xt", "xtz"], ["qx"])
+    op("g", lambda e: e.partition_broadcast(T.strb[:], T.str1[0:1, 0:A], 128), ["str1"], ["strb"])
+    send("wide_c", lambda d: codes("qx", 0, A), lambda d: codes("lx0", A * rank, A * rank + A), ["qx"])
+    send("wide_s", lambda d: T.qxs[:, 0:A], lambda d: T.lx0s[:, A * rank:A * rank + A], ["qx"])
+    dma("s", "own0", codes("lx0", A * rank, A * rank + A), codes("qx", 0, A), ["qx"], ["lx0own"])
+    dma("s", "own0", T.lx0s[:, A * rank:A * rank + A], T.qxs[:, 0:A], ["qx"], ["lx0own2"])
+    dma("s", "w", T.wt[:], T.w[:], [], ["wt"])
+
+    def to_table(k, src, out, key):
+        e, et, u = T.e, T.et, T.u
+        ts(e[:], T.mm[:, 0:32], src[:, 0:1], ALU.mult, ["mm", key], ["e"])
+        op("v", lambda v: v.transpose(et[:], e[:]), ["e"], ["et"])
+        yield
+        for i in range(4):
+            red(u[:, i:i + 1], et[:, 16 * (i % 2):16 * (i % 2) + 16], ["et"], ["u%d" % i])
+        for h in (0, 64):
+            cp(u[h + 32:h + 64, 0:2], u[h:h + 32, 0:2], ["u0", "u1"], ["uw%d" % h])
+            cp(u[h:h + 32, 2:4], u[h + 32:h + 64, 2:4], ["u2", "u3"], ["uv%d" % h])
+        for h in (0, 64):
+            for o in (0, 64):
+                cp(out[o:o + 64, h // 16:h // 16 + 4], u[h:h + 64, 0:4],
+                   ["u0", "u1", "u2", "u3", "uw%d" % h, "uv%d" % h], ["tab" + k + "%d%d" % (h, o)])
+        yield
+
+    def tab(k):
+        return ["tab%s%d%d" % (k, h, o) for h in (0, 64) for o in (0, 64)]
+
+    def lists(t):
+        n = str(t)
+        ts(T["dr" + n][:], T["nri" + n][:], 6, ALU.arith_shift_right, ["nri" + n], ["dr" + n])
+        ts(T.vv[:], T["nri" + n][:], 63, ALU.bitwise_and, ["nri" + n], ["vv"])
+        ts(T.eq[:], T["dr" + n][:], T.pdf[:, 0:1], ALU.is_equal, ["dr" + n, "pdf"], ["eq"])
+        tt(T.xx[:, 0:A], T.vv[:], T["loc64" + n][:], ALU.add, ["vv", "loc64" + n], ["xx"])
+        op("v", lambda e: e.tensor_tensor_scan(T.cum[:], T.one[:], T.eq[:], 0.0, ALU.mult, ALU.add), ["one", "eq"], ["cum"])
+        tt(T.dx[:], T.xx[:, 1:A + 1], T.xx[:, 0:A], ALU.subtract, ["xx", "xxz"], ["dx"])
+        ts(T.lt[:], T.cum[:], T.r1[:, 0:1], ALU.is_lt, ["cum", "r1"], ["lt"])
+        cp(T.pr[:, A:A + 1], T.xx[:, 0:1], ["xx"], ["prz"])
+        tt(T.pr[:, 0:A], T.lt[:], T.dx[:], ALU.mult, ["lt", "dx"], ["pr"])
+        red(T.xs[:], T.pr[:], ["pr", "prz"], ["xs"])
+        k = "l" + n
+        for _ in to_table(k, T.xs, T["ti" + n], "xs"):
+            pass
+        x = T["xr" + n]
+        send("xr" + n, lambda d: T["ti" + n][:, d:d + 1], lambda d: x[:, 4 * rank:4 * rank + 1], tab(k))
+        ts(T["shx" + n][:], T["ti" + n][:], 6, ALU.arith_shift_right, tab(k), ["shx" + n])
+
+    def received(t):
+        n = str(t)
+        xv = T["xr" + n][:, 0:4 * N:4]
+        src = ["in_xr" + n, "xrown" + n]
+        if t == 0:
+            ts(T.lsh[:], xv, 6, ALU.arith_shift_right, src, ["lsh"])
+        ts(T.vi[:], xv, 63, ALU.bitwise_and, src, ["vi"])
+        if t == 0:
+            tt(T.lsa[:], T.lsh[:], T.fs[:], ALU.mult, ["lsh", "fs"], ["lsa"])
+        tt(T.vm[:], T.vi[:], T.blk[:], ALU.mult, ["vi", "blk"], ["vm"])
+        if t == 0:
+            tt(T.lsa[:], T.lsa[:], T.cc[:], ALU.add, ["lsa", "cc"], ["lsa"])
+        red(T.v[:], T.vm[:], ["vm"], ["v"])
+        if t == 0:
+            cp(T.lsu[:], T.lsa[:], ["lsa"], ["lsu"])
+        ts(T.zlf[:], T.ibq[:], T.v[:, 0:1], ALU.add, ["ibq", "v"], ["zlf"], 4.0, ALU.mult)
+        ts(T.ll[:, 3:4], T.v[:], 4.0, ALU.mult, ["v"], ["llz"])
+        cp(T["zl" + n][:], T.zlf[:], ["zlf"], ["zl" + n])
+        if t == 0:
+            pick("land0", 0, "lx0", 256, T.lsu[:, 0:8], 128, ["in_lx0", "lx0own", "lx0own2", "lsu"], "land0")
+        tt(T.ng[:], T.nxf[:, 0:P].indirect(T["zl" + n][:, 0:4]), T.mm[:], ALU.mult, ["nxf", "zl" + n, "mm"], ["ng"])
+        for b in range(4):
+            red(T.n4[:, b:b + 1], T.ng[:, 16 * b:16 * b + 16], ["ng"], ["n4%d" % b])
+        n4 = ["n4%d" % b for b in range(4)]
+        tt(T.dn[:], T.n4[:, 1:4], T.n4[:, 0:3], ALU.subtract, n4, ["dn"])
+        cp(T.npr[:, 3:4], T.n4[:, 0:1], n4, ["npz"])
+
+    def serve(t):
+        n = str(t)
+        land, nt = "land" + n, T["nt" + n]
+        lk = ["land0_c", "land0_s"] if t == 0 else ["in_land1", "land1own", "land1own2"]
+        mx(0, P, land, 0, "kq", 0, lk + ["kq"])
+        for i in range(4):
+            mx(1 + i, 128, "h", 128 * i, land, 0, lk + ["h%d" % i])
+        act(T.zs[:], bank(0, P), ["bank0"], ["zs"])
+        for i in range(4):
+            act(T.dq[:, 128 * i:128 * i + 128], bank(1 + i, 128), ["bank%d" % (1 + i)], ["dq%d" % i])
+        tt(T.zg[:], T.zs[:, 0:P].indirect(T["zl" + n][:, 0:4]), T.dm[:], ALU.add, ["zs", "zl" + n, "dm"], ["zg"])
+        op("v", lambda e: e.tensor_tensor_scan(T.rm[:], T.zg[:], T.zg[:], -2e29, ALU.max, ALU.max), ["zg"], ["rm"])
+        ts(T.ll[:, 0:3], T.rm[:, 15:48:16], T.rm[:, 63:64], ALU.is_lt, ["rm"], ["ll"])
+        red(T.c[:], T.ll[:], ["ll", "llz"], ["c"])
+        tt(T.npr[:, 0:3], T.ll[:, 0:3], T.dn[:], ALU.mult, ["ll", "dn"], ["npr"])
+        k = "s" + n
+        steps = to_table(k, T.c, T.ct, "c")
+        next(steps)
+        red(T["node" + n][:], T.npr[:], ["npr", "npz"], ["node" + n])
+        next(steps)
+        send("rn" + n, lambda d: T["node" + n][:], lambda d: T["rn" + n][:, rank:rank + 1], ["node" + n])
+        dma("s", "rnown" + n, T["rn" + n][:, rank:rank + 1], T["node" + n][:], ["node" + n], ["rnown" + n])
+        for i in range(4):
+            tt(nt[:, i:512:4], T.hk[:, P * i:P * i + P].indirect(T.ct[:, 0:8]), T.dq[:, 128 * i:128 * i + 128], ALU.add,
+               ["hk%d" % i, "dq%d" % i] + tab(k), ["nt%s%d" % (n, i)])
+        quant("new" + n, 0, 128, nt[:], ["nt%s%d" % (n, i) for i in range(4)], ["new" + n])
+        win, at = ("wina", 128) if t == 0 else ("winb", A)
+        at += CAPP * rank
+        send("ret%s_c" % n, lambda d: codes("new" + n, CAPP * d, CAPP * d + CAPP), lambda d: codes(win, at, at + CAPP), ["new" + n])
+        send("ret%s_s" % n, lambda d: T["new%ss" % n][:, CAPP * d:CAPP * d + CAPP], lambda d: T[win + "s"][:, at:at + CAPP], ["new" + n])
+        dma("a", "self" + n, codes(win, at, at + CAPP), codes("new" + n, CAPP * rank, CAPP * rank + CAPP), ["new" + n], [win + "own"])
+        dma("a", "self" + n, T[win + "s"][:, at:at + CAPP], T["new%ss" % n][:, CAPP * rank:CAPP * rank + CAPP], ["new" + n], [win + "own2"])
+        dma("s", "row" + n, T["row" + n][0:1, :], T["rn" + n][CAPP * rank:CAPP * rank + CAPP, 0:N], ["in_rn" + n, "rnown" + n], ["row" + n])
+        op("g", lambda e: e.partition_broadcast(T["mrs" + n][:, A:A + 128], T["row" + n][0:1, :], 128), ["row" + n], ["mrsr" + n])
+
+    def slotmap(t):
+        n = str(t)
+        dr = T["dr" + n]
+        for d in range(N):
+            ts(T.e8[:, A * d:A * d + A], dr[:], float(d), ALU.is_equal, ["dr" + n], ["e8%d" % d])
+        e8 = ["e8%d" % d for d in range(N)]
+        op("v", lambda e: e.tensor_tensor_scan(T.c8[:], T.rst[:], T.e8[:], 0.0, ALU.mult, ALU.add), e8 + ["rst"], ["c8"])
+        base = 128 if t == 0 else A
+        ts(T.ta[:], dr[:], 16.0, ALU.mult, ["dr" + n], ["ta"], float(base - 1), ALU.add)
+        tt(T.c8[:], T.c8[:], T.e8[:], ALU.mult, e8 + ["c8"], ["c8"])
+        tt(T.nb[:], dr[:], T.af[:], ALU.subtract, ["dr" + n, "af"], ["nb"])
+        tt(T.c8[:, 0:128], T.c8[:, 0:128], T.c8[:, 128:256], ALU.add, ["c8"], ["c8"])
+        tt(T.c8[:, 0:64], T.c8[:, 0:64], T.c8[:, 64:128], ALU.add, ["c8"], ["c8"])
+        tt(T.rk[:], T.c8[:, 0:32], T.c8[:, 32:64], ALU.add, ["c8"], ["rk"])
+        ts(T.sv[:], T.rk[:], float(CAPP), ALU.is_le, ["rk"], ["sv"])
+        ts(T.na[:], T.rk[:], 8.0, ALU.mult, ["rk"], ["na"], float(A - 8), ALU.add)
+        tt(T.tb[:], T.rk[:], T.af[:], ALU.subtract, ["rk", "af"], ["tb"])
+        tt(T.na[:], T.na[:], T.nb[:], ALU.add, ["na", "nb"], ["na"])
+        tt(T.ta[:], T.ta[:], T.tb[:], ALU.add, ["ta", "tb"], ["ta"])
+        tt(T.na[:], T.na[:], T.sv[:], ALU.mult, ["na", "sv"], ["na"])
+        tt(T.ta[:], T.ta[:], T.sv[:], ALU.mult, ["ta", "sv"], ["ta"])
+        tt(T.na[:], T.na[:], T.af[:], ALU.add, ["na", "af"], ["na"])
+        tt(T.ta[:], T.ta[:], T.af[:], ALU.add, ["ta", "af"], ["ta"])
+        tt(T.nb[:], T.na[:], T.mm[:, 0:A], ALU.mult, ["na", "mm"], ["nb"])
+        tt(T.tb[:], T.ta[:], T.mm[:, 0:A], ALU.mult, ["ta", "mm"], ["tb"])
+        for h in range(2):
+            red(T.n2[:, h:h + 1], T.nb[:, 16 * h:16 * h + 16], ["nb"], ["n2%d" % h])
+            red(T.l2[:, h:h + 1], T.tb[:, 16 * h:16 * h + 16], ["tb"], ["l2%d" % h])
+        if t == 0:
+            ts(T.loc641[:], T.ta[:], 64.0, ALU.mult, ["ta"], ["loc641"])
+        cp(T["nu" + n][:], T.n2[:], ["n20", "n21"], ["nu" + n])
+        cp(T["lu" + n][:], T.l2[:], ["l20", "l21"], ["lu" + n])
+
+    cp(T.nri0[:, 0:16], T.strb[:, 0:A:2], ["strb"], ["nri0"])
+    cp(T.nri0[:, 16:32], T.strb[:, 1:A:2], ["strb"], ["nri0"])
+    lists(0)
+    for i, c in enumerate(picked):
+        d = cores.index(c)
+        cp(T.pl[:, i:i + 1], T.shx0[:, d:d + 1], ["shx0"], ["pl%d" % i])
+    pick("send0", 0, "qx", 128, T.pl[:, 0:2], 32, ["qx", "pl0", "pl1"], "send0")
+    slot = {cores.index(c): i * CAPP for i, c in enumerate(picked)}
+    send("pick_c", lambda d: codes("send0", slot[d], slot[d] + CAPP), lambda d: codes("lx0", A * rank, A * rank + CAPP), ["send0_c"])
+    send("pick_s", lambda d: T.send0s[:, slot[d]:slot[d] + CAPP], lambda d: T.lx0s[:, A * rank:A * rank + CAPP], ["send0_s"])
+    cp(T.xr0[:, 4 * rank:4 * rank + 1], T.ti0[:, rank:rank + 1], tab("l0"), ["xrown0"])
+    op("g", lambda e: e.partition_broadcast(T.nxr[:], T.nx1[0:1, :], 128), ["nx1"], ["nxr"])
+    quant("kq", 0, P, T.kt[:], ["kt"], ["kq"])
+    for i in range(4):
+        quant("h", 128 * i, 128 * i + 128, T.hb[:, 3 - i:515 - i], ["hb"], ["h%d" % i])
+        mx(1 + i, P, "h", 128 * i, "kq", 0, ["kq", "h%d" % i])
+        act(T.hk[:, P * i:P * i + P], bank(1 + i, P), ["bank%d" % (1 + i)], ["hk%d" % i])
+    ts(T.j15[:, 0:16], T.p15[:, 0:16], 16.0, ALU.mult, ["p15"], ["j15"])
+    tt(T.j15[:, 0:16], T.j15[:, 0:16], T.ioj[:, 0:16], ALU.add, ["j15", "ioj"], ["j15"])
+    cp(T.pi[:], T.j15[:, 0:16], ["j15"], ["pi"])
+    cp(T.nxf[:], T.nxr[:, 0:P].indirect(T.pi[:, 0:16]), ["nxr", "pi"], ["nxf"])
+    received(0)
+    serve(0)
+    fill(T.rst[:], 1.0, ["rst"])
+    fill(T.rst[:, 0:256:32], 0.0, ["rst"])
+    cp(T.af[:], T.ioj[:, 0:A], ["ioj"], ["af"])
+    cp(T.mrs0[:, 0:A], T.nri0[:], ["nri0"], ["mrsq0"])
+    slotmap(0)
+    quant("wina", 0, 128, T.xt[:], ["xt", "xtz"], ["winaq"])
+    cp(T.nri1[:], T.mrs0[:, 0:160].indirect(T.nu0[:, 0:2]), ["mrsq0", "mrsr0", "nu0"], ["nri1"])
+    lists(1)
+    cp(T.sl[:], T.shx1[:], ["shx1"], ["sl"])
+    cp(T.xr1[:, 4 * rank:4 * rank + 1], T.ti1[:, rank:rank + 1], tab("l1"), ["xrown1"])
+    wina = ["winaq", "winaown", "winaown2", "in_ret0"]
+    pick("send1", 0, "wina", 256, T.sl[:, 0:8], 128, wina + ["sl"], "send1")
+    at = CAPP * rank
+    send("land1_c", lambda d: codes("send1", CAPP * d, CAPP * d + CAPP), lambda d: codes("land1", at, at + CAPP), ["send1_c"])
+    send("land1_s", lambda d: T.send1s[:, CAPP * d:CAPP * d + CAPP], lambda d: T.land1s[:, at:at + CAPP], ["send1_s"])
+    dma("s", "own1", codes("land1", at, at + CAPP), codes("send1", at, at + CAPP), ["send1_c"], ["land1own"])
+    dma("s", "own1", T.land1s[:, at:at + CAPP], T.send1s[:, at:at + CAPP], ["send1_s"], ["land1own2"])
+    cp(T.mrs1[:, 0:A], T.nri1[:], ["nri1"], ["mrsq1"])
+    dma("s", "nd0", T.nd[0:1, :], T.mrs0[0:1, 0:A], ["mrsq0"], [])
+    dma("s", "nd1", T.nd[1:2, :], T.mrs1[0:1, 0:A], ["mrsq1"], [])
+    received(1)
+    serve(1)
+    slotmap(1)
+    pick("winb", 0, "wina", 256, T.lu0[:, 0:2], A, wina + ["lu0"], "winbq")
+    quant("wq", 0, 128, T.wt[:], ["wt"], ["wq"])
+    quant("fin", 0, 128, T.xt[:], ["xt", "xtz"], ["fin_c", "fin_s"])
+    pick("fin", 0, "winb", 160, T.lu1[:, 0:2], A, ["winbq_c", "winbq_s", "winbown", "winbown2", "in_ret1", "lu1"], "fin")
+    mx(5, 128, "wq", 0, "fin", 0, ["wq", "fin_c", "fin_s"])
+    act(T.ys[:], bank(5, A), ["bank5"], ["ys"])
+    dma("a", "y", T.y[:], T.ys[:], ["ys"], [])
+    dma("s", "oc", T.oc[:], codes("fin", 0, A), ["fin_c"], [])
+    for k in range(4):
+        dma("s" if k % 2 else "a", "osc", T.osc[4 * k:4 * k + 4, :], T.fins[32 * k:32 * k + 4, 0:A], ["fin_s"], [])
+    cp(T.nr2[:], T.mrs1[:, 0:160].indirect(T.nu1[:, 0:2]), ["mrsq1", "mrsr1", "nu1"], ["nr2"])
+    dma("s", "nd2", T.nd[2:3, :], T.nr2[0:1, :], ["nr2"], [])
+    g.wait_ge(T.sem.left, left[0])
+    for q, s in sems.items():
+        g.wait_ge(T.sem[s], count[q])
+    for s, v in dcount.items():
+        g.wait_ge(T.sem[s], v)

@@ -3,7 +3,7 @@ from concourse.mybir import dt, AluOpType, AxisListType, ActivationFunctionType
 
 N, P, A, CAPP = 8, 256, 32, 16
 F8, U8, F32, BF, I32, U16 = "float8_e4m3fn_x4", "uint8", "float32", "bfloat16", "int32", "uint16"
-
+BIG = 32 * 16384
 SCRATCH = {}
 
 
@@ -11,37 +11,32 @@ def _add(name, cols, dtype, where="sbuf"):
     SCRATCH[name] = (where, [128, cols], dtype)
 
 
-def _pair(name, cols):
-    _add(name + "c", cols, F8)
-    _add(name + "s", cols, U8)
-
-
-for _n, _c in (("qx", 128), ("lx0", 256), ("send0", 32), ("land0", 128), ("new0", 128), ("wina", 256), ("send1", 128),
-               ("land1", 128), ("new1", 128), ("winb", 160), ("fin", 128), ("kq", 256), ("wq", 128), ("h", 512)):
-    _pair(_n, _c)
-for _n, _c, _d in (("xt", 512, BF), ("kt", 1024, BF), ("wt", 512, BF), ("hr", 516, BF), ("hb", 516, BF), ("hk", 1024, BF),
-                   ("iop", 64, I32), ("ioj", 64, I32), ("p15", 64, I32), ("pd", 64, I32), ("j15", 64, I32), ("mm", 64, F32),
-                   ("dm", 64, F32), ("blk", 8, F32), ("pdf", 1, F32), ("r1", 1, F32), ("ibq", 4, F32), ("af", 32, F32),
-                   ("pi", 16, U16), ("rst", 256, F32), ("fs", 8, F32), ("cc", 8, F32), ("one", 32, F32),
-                   ("str1", 32, I32), ("strb", 32, I32), ("nx1", 256, I32), ("nxr", 256, I32), ("nxf", 256, F32),
-                   ("lsh", 8, I32), ("lsa", 8, F32), ("lsu", 8, U16),
-                   ("pl", 2, U16), ("sl", 8, U16), ("nr2", 32, F32), ("ys", 32, F32),
-                   ("vv", 32, I32), ("xx", 33, F32), ("dx", 32, F32), ("eq", 32, F32), ("cum", 32, F32), ("lt", 32, F32),
-                   ("pr", 33, F32), ("xs", 1, F32), ("vi", 8, I32), ("vm", 8, F32), ("v", 1, F32), ("zlf", 4, F32),
-                   ("ng", 64, F32), ("n4", 4, F32), ("dn", 3, F32), ("zs", 256, F32), ("zg", 64, F32), ("rm", 64, F32),
-                   ("ll", 4, F32), ("c", 1, F32), ("npr", 4, F32), ("ct", 8, U16), ("dq", 512, F32),
-                   ("e8", 256, F32), ("c8", 256, F32), ("rk", 32, F32), ("sv", 32, F32), ("ta", 32, F32), ("tb", 32, F32),
-                   ("l2", 2, F32), ("na", 32, F32), ("nb", 32, F32), ("n2", 2, F32), ("e", 32, F32), ("et", 32, F32), ("u", 4, F32)):
+for _n, _c in (("qx", 128), ("lx0", 256), ("send0", 32), ("land0", 128), ("new0", 128), ("wina", 160), ("send1", 128),
+               ("land1", 128), ("new1", 128), ("winb", 160), ("fin", 128), ("kq", 256), ("wq", 128), ("h", 512), ("ws", 128),
+               ("kp0", 128), ("kp1", 128), ("xq0", 128), ("xq1", 128)):
+    _add(_n + "c", _c, F8)
+    _add(_n + "s", _c, U8)
+for _n, _c, _d in (("xt", 512, BF), ("kt", 1024, BF), ("wt", 512, BF), ("hb", 516, BF), ("wb", 512, BF), ("xb", 512, BF),
+                   ("iop", 8, I32), ("ioj", 32, I32), ("jmp", 128, I32), ("xa0", 32, F32), ("xa1", 32, F32),
+                   ("el", 8, I32), ("elst", 8, U16), ("locrow", 128, F32), ("rowc", 128, F32), ("io16", 8, I32), ("slott", 8, F32),
+                   ("pd", 8, I32), ("mm", 128, F32), ("dm", 64, F32), ("blk", 8, F32), ("bki", 8, F32),
+                   ("r1", 1, F32), ("ibq", 4, F32), ("dcol", 4, F32), ("rst", 128, BF), ("rs2", 128, F32),
+                   ("fs", 8, F32), ("cc", 8, F32), ("str1", 32, I32), ("strb", 32, I32), ("nd0f", 32, F32),
+                   ("nxt", 32, I32), ("nxh", 32, I32), ("nxp", 32, F32), ("nxq", 32, F32), ("nx1", 256, F32), ("nxf", 256, F32),
+                   ("lsu", 8, U16), ("pl", 2, U16), ("sl", 8, U16), ("ol", 2, U16), ("ys", 32, F32),
+                   ("dr", 32, I32), ("xm", 32, I32), ("xx", 32, F32), ("shx", 8, I32), ("zl", 4, U16), ("ct", 8, U16),
+                   ("win", 160, F32), ("lu", 8, U16), ("so", 160, F32), ("dn", 32, F32), ("dl", 32, I32),
+                   ("vi", 8, I32), ("vm", 8, F32), ("v", 1, F32), ("v4", 8, F32), ("zlf", 4, F32), ("zs", 256, F32), ("zg", 64, F32), ("rm", 64, F32),
+                   ("eqb", 128, BF), ("cum", 128, BF), ("yy", 128, F32), ("mn", 128, F32),
+                   ("ia", 8, I32), ("fl", 8, F32), ("n2", 2, F32)):
     _add(_n, _c, _d)
 for _t in ("0", "1"):
-    for _n, _c, _d in (("nri", 32, I32), ("dr", 32, I32), ("loc64", 32, F32), ("ti", 8, I32), ("shx", 8, I32), ("xr", 32, I32),
-                       ("zl", 4, U16), ("node", 1, F32), ("nt", 512, BF), ("rn", 8, F32), ("row", 128, F32), ("mrs", 160, F32),
-                       ("lu", 2, U16), ("nu", 2, U16)):
+    for _n, _c, _d in (("ti", 8, I32), ("xr", 32, I32), ("nodt", 128, F32), ("nt", 512, BF), ("rn", 32, F32),
+                       ("vv", 32, I32), ("nu", 2, U16), ("ndf", 32, F32)):
         _add(_n + _t, _c, _d)
-_add("bank", 512 * 6, F32, "psum")
-
+_add("bank", 512 * 8, F32, "psum")
 ARRIVE = ["lx0", "xr0", "rn0", "ret0", "xr1", "land1", "rn1", "ret1"]
-DMAS = ["st", "x", "ky", "nx", "w", "own0", "nd0", "rnown0", "rnown1", "row0", "row1", "self0", "self1", "own1", "nd1", "nd2", "oc", "osc", "y"]
+DMAS = ["st", "x", "ky", "nx", "w", "nxr", "own0", "ownw", "nd0", "nd1", "nd2", "oc", "osc", "y"]
 SEMAPHORES = ["sg", "sv", "sa", "sp", "left"] + ["a_" + k for k in ARRIVE] + ["d_" + k for k in DMAS]
 
 
@@ -98,13 +93,14 @@ def rank_program(g, core, T, topo):
     if rank is None:
         return
     cores = list(T.cores)
-    others = [c for c in cores if c != core]
+    odd = rank % 2
     plans = {c: _plan(topo, cores, c) for c in cores}
     calls, picked, wide = plans[core]
     want = {k: 0 for k in ARRIVE}
-    for c in others:
-        for k, a in ROUTE.items():
-            want[a] += _bits(plans[c][0][k].get(core, 0))
+    for c in cores:
+        if c != core:
+            for k, a in ROUTE.items():
+                want[a] += _bits(plans[c][0][k].get(core, 0))
     ALU, X, CP = AluOpType, AxisListType.X, ActivationFunctionType.Copy
     queues = {"g": g, "v": g.vector, "a": g.scalar, "p": g.tensor, "s": g.sync}
     sems = {"g": "sg", "v": "sv", "a": "sa", "p": "sp"}
@@ -164,8 +160,8 @@ def rank_program(g, core, T, topo):
         tr = []
         for c, m in calls[call].items():
             rid, pid = topo.addr(c, core)
-            tr.append(RemoteDMATransfer(dst_ids=[DstId(rid=rid, pnc=pid)], dma_engine_mask=m, remote_sem=T.sem["a_" + ROUTE[call]],
-                                        src=src(cores.index(c)), dst=dst(cores.index(c))))
+            d = cores.index(c)
+            tr.append(RemoteDMATransfer(dst_ids=[DstId(rid=rid, pnc=pid)], dma_engine_mask=m, remote_sem=T.sem["a_" + ROUTE[call]], src=src(d), dst=dst(d)))
             left[0] += _bits(m)
         g.remote_dma_fused(tr, local_sem=T.sem.left)
 
@@ -193,15 +189,27 @@ def rank_program(g, core, T, topo):
     def red(out, a, reads, writes, o=ALU.add):
         op("v", lambda e: e.tensor_reduce(out, a, X, o), reads, writes)
 
+    def scan(out, a, b, init, o0, o1, reads, writes):
+        op("v", lambda e: e.tensor_tensor_scan(out, a, b, init, o0, o1), reads, writes)
+
+    def turn(out, a, reads, writes):
+        op("v", lambda e: e.transpose(out, a), reads, writes)
+
     def fill(ap, value, writes):
         op("v", lambda e: e.memset(ap, value), [], writes)
 
     def quant(name, a, b, tile, reads, writes):
         op("v", lambda e: e.quantize_mx(T[name + "c"][:, a:b], T[name + "s"][:, a:b], tile), reads, writes)
 
-    def mx(bank, n, l, la, r, ra, reads):
+    def iota(out, pattern, base, step, writes, flag=False):
+        if flag:
+            op("g", lambda e: e.iota(out, pattern, base, step, allow_small_or_imprecise_dtypes=True), [], writes)
+        else:
+            op("g", lambda e: e.iota(out, pattern, base, step), [], writes)
+
+    def mx(bank, n, l, la, r, ra, reads, start=True, stop=True):
         op("p", lambda e: e.matmul_mx(T.bank[:, 512 * bank:512 * bank + n], T[l + "c"][:, la:la + 128], T[l + "s"][:, la:la + 128],
-                                      T[r + "c"][:, ra:ra + n], T[r + "s"][:, ra:ra + n], True, True), reads, ["bank%d" % bank])
+                                      T[r + "c"][:, ra:ra + n], T[r + "s"][:, ra:ra + n], start, stop), reads, ["bank%d" % bank])
 
     def bank(k, n):
         return T.bank[:, 512 * k:512 * k + n]
@@ -209,237 +217,261 @@ def rank_program(g, core, T, topo):
     def act(out, in_, reads, writes):
         op("a", lambda e: e.activation(out, in_, CP), reads, writes)
 
+    def zero(out, in_, reads, writes):
+        op("a", lambda e: e.activation(out, in_, CP, scale=0.0), reads, writes)
+
     def pick(out, oa, win, wb, off, n, reads, key):
         cp(words(out, oa, oa + n), words(win, 0, wb).indirect(off), reads, [key + "_c"])
         act(T[out + "s"][:, oa:oa + n], T[win + "s"][:, 0:wb].indirect(off), reads, [key + "_s"])
 
+    def place(r):
+        return r ^ odd
+
+    def seen(r):
+        return rank ^ (r % 2)
+
+    me = place(rank)
+    mine = CAPP * me
     dma("s", "st", T.str1[0:1, 0:A], T.st[:], [], ["str1"])
     dma("a", "x", T.xt[:, 0:4 * A], T.x[:], [], ["xt"])
     dma("s", "ky", T.kt[:], T.ky[:], [], ["kt"])
-    dma("a", "nx", T.nx1[0:1, 0:P], T.nx[:], [], ["nx1"])
-    op("g", lambda e: e.iota(T.iop[:], [[0, 64]], 0, 1), [], ["iop"])
-    op("g", lambda e: e.iota(T.ioj[:], [[1, 64]], 0, 0), [], ["ioj"])
-    fill(T.hr[:], 0.5, ["hr"])
+    fill(T.nxt[0:32, :], 0, ["nxt"])
+    iota(T.jmp[:], [[1, 128]], 0, -1, ["jmp"])
+    iota(T.iop[:], [[0, 8]], 0, 1, ["iop"])
+    iota(T.ioj[:], [[1, A]], 0, 0, ["ioj"])
+    iota(T.xa0[:], [[16384 + 64, A]], 0, 0, ["xa0"], True)
+    dma("a", "nx", T.nxt[0:16, 0:16], T.nx[:], ["nxt"], ["nxt"])
     fill(T.xt[:, 4 * A:512], 0.0, ["xtz"])
-    op("g", lambda e: e.affine_select(T.hb[:], T.hr[:], [[-1, 516]], ALU.is_equal, 0.0, 3, 4), ["hr"], ["hb"])
-    ts(T.p15[:], T.iop[:], 15, ALU.bitwise_and, ["iop"], ["p15"])
-    ts(T.pd[:], T.iop[:], 4, ALU.arith_shift_right, ["iop"], ["pd"])
-    ts(T.j15[:], T.ioj[:], 15, ALU.bitwise_and, ["ioj"], ["j15"])
-    fill(T.one[:], 1.0, ["one"])
-    cp(T.pdf[:], T.pd[:, 0:1], ["pd"], ["pdf"])
-    ts(T.r1[:], T.p15[:, 0:1], 1.0, ALU.add, ["p15"], ["r1"])
-    tt(T.mm[:], T.p15[:], T.j15[:], ALU.is_equal, ["p15", "j15"], ["mm"])
-    ts(T.loc640[:], T.ioj[:, 0:A], 64.0, ALU.mult, ["ioj"], ["loc640"])
-    fill(T.xx[:, A:A + 1], 0.0, ["xxz"])
-    tt(T.blk[:], T.pd[:, 0:N], T.ioj[:, 0:N], ALU.is_equal, ["pd", "ioj"], ["blk"])
-    ts(T.ibq[:], T.ioj[:, 0:4], 0.25, ALU.mult, ["ioj"], ["ibq"])
-    ts(T.dm[:], T.mm[:], -1.0, ALU.add, ["mm"], ["dm"], 1e29, ALU.mult)
-    fill(T.fs[:], 1.0, ["fs"])
-    ts(T.cc[:], T.ioj[:, 0:N], 32.0, ALU.mult, ["ioj"], ["cc"])
-    for s, c in enumerate(cores):
-        if c != core and core in plans[c][1]:
-            fill(T.fs[:, s:s + 1], 0.0, ["fs"])
-            ts(T.cc[:, s:s + 1], T.p15[:, 0:1], float(32 * s), ALU.add, ["p15"], ["cc"])
-
+    fill(T.hb[:], 0.0, ["hb"])
+    dcol = []
+    for q in range(4):
+        for half in range(2):
+            dcol.append("dcol%d%d" % (q, half))
+            fill(T.dcol[64 * half:64 * half + 64, q:q + 1], float(place(4 * half + q)), dcol[-1:])
+    ts(T.hb[:, 3:515:4], T.jmp[:], 0.0, ALU.is_equal, ["jmp"], ["hb"], 0.5, ALU.mult)
+    ts(T.ia[:], T.iop[:], 15, ALU.bitwise_and, ["iop"], ["ia"])
+    fill(T.rst[:], 1.0, ["rst"])
+    fill(T.rst[:, 0:128:32], 0.0, ["rst"])
+    fill(T.rs2[:], 0.0, ["rs2"])
+    fill(T.rs2[:, 0:128:32], float(4 * BIG), ["rs2"])
+    ts(T.r1[:], T.ia[:, 0:1], 1.0, ALU.add, ["ia"], ["r1"])
+    ts(T.jmp[:], T.jmp[:], 15, ALU.bitwise_and, ["jmp"], ["jmp"])
+    ts(T.mm[:], T.jmp[:], 0.0, ALU.is_equal, ["jmp"], ["mm"])
+    zero(T.xb[:], T.hb[:, 0:512], ["hb"], ["xbz"])
+    zero(T.wb[:], T.hb[:, 0:512], ["hb"], ["wb"])
     quant("qx", 0, 128, T.xt[:], ["xt", "xtz"], ["qx"])
     op("g", lambda e: e.partition_broadcast(T.strb[:], T.str1[0:1, 0:A], 128), ["str1"], ["strb"])
-    send("wide_c", lambda d: codes("qx", 0, A), lambda d: codes("lx0", A * rank, A * rank + A), ["qx"])
-    send("wide_s", lambda d: T.qxs[:, 0:A], lambda d: T.lx0s[:, A * rank:A * rank + A], ["qx"])
-    dma("s", "own0", codes("lx0", A * rank, A * rank + A), codes("qx", 0, A), ["qx"], ["lx0own"])
-    dma("s", "own0", T.lx0s[:, A * rank:A * rank + A], T.qxs[:, 0:A], ["qx"], ["lx0own2"])
-    dma("s", "w", T.wt[:], T.w[:], [], ["wt"])
-
-    def to_table(k, src, out, key):
-        e, et, u = T.e, T.et, T.u
-        ts(e[:], T.mm[:, 0:32], src[:, 0:1], ALU.mult, ["mm", key], ["e"])
-        op("v", lambda v: v.transpose(et[:], e[:]), ["e"], ["et"])
-        yield
-        for i in range(4):
-            red(u[:, i:i + 1], et[:, 16 * (i % 2):16 * (i % 2) + 16], ["et"], ["u%d" % i])
-        for h in (0, 64):
-            cp(u[h + 32:h + 64, 0:2], u[h:h + 32, 0:2], ["u0", "u1"], ["uw%d" % h])
-            cp(u[h:h + 32, 2:4], u[h + 32:h + 64, 2:4], ["u2", "u3"], ["uv%d" % h])
-        for h in (0, 64):
-            for o in (0, 64):
-                cp(out[o:o + 64, h // 16:h // 16 + 4], u[h:h + 64, 0:4],
-                   ["u0", "u1", "u2", "u3", "uw%d" % h, "uv%d" % h], ["tab" + k + "%d%d" % (h, o)])
-        yield
+    send("wide_c", lambda d: codes("qx", 0, A), lambda d: codes("lx0", A * seen(d), A * seen(d) + A), ["qx"])
+    send("wide_s", lambda d: T.qxs[:, 0:A], lambda d: T.lx0s[:, A * seen(d):A * seen(d) + A], ["qx"])
+    dma("s", "own0", codes("lx0", A * me, A * me + A), codes("qx", 0, A), ["qx"], ["lx0own"])
+    dma("s", "own0", T.lx0s[:, A * me:A * me + A], T.qxs[:, 0:A], ["qx"], ["lx0own2"])
 
     def tab(k):
-        return ["tab%s%d%d" % (k, h, o) for h in (0, 64) for o in (0, 64)]
+        return ["tab%s%d%d" % (k, a, b) for a in range(2) for b in range(2)]
 
     def lists(t):
         n = str(t)
-        ts(T["dr" + n][:], T["nri" + n][:], 6, ALU.arith_shift_right, ["nri" + n], ["dr" + n])
-        ts(T.vv[:], T["nri" + n][:], 63, ALU.bitwise_and, ["nri" + n], ["vv"])
-        ts(T.eq[:], T["dr" + n][:], T.pdf[:, 0:1], ALU.is_equal, ["dr" + n, "pdf"], ["eq"])
-        tt(T.xx[:, 0:A], T.vv[:], T["loc64" + n][:], ALU.add, ["vv", "loc64" + n], ["xx"])
-        op("v", lambda e: e.tensor_tensor_scan(T.cum[:], T.one[:], T.eq[:], 0.0, ALU.mult, ALU.add), ["one", "eq"], ["cum"])
-        tt(T.dx[:], T.xx[:, 1:A + 1], T.xx[:, 0:A], ALU.subtract, ["xx", "xxz"], ["dx"])
-        ts(T.lt[:], T.cum[:], T.r1[:, 0:1], ALU.is_lt, ["cum", "r1"], ["lt"])
-        cp(T.pr[:, A:A + 1], T.xx[:, 0:1], ["xx"], ["prz"])
-        tt(T.pr[:, 0:A], T.lt[:], T.dx[:], ALU.mult, ["lt", "dx"], ["pr"])
-        red(T.xs[:], T.pr[:], ["pr", "prz"], ["xs"])
-        k = "l" + n
-        for _ in to_table(k, T.xs, T["ti" + n], "xs"):
-            pass
-        x = T["xr" + n]
-        send("xr" + n, lambda d: T["ti" + n][:, d:d + 1], lambda d: x[:, 4 * rank:4 * rank + 1], tab(k))
-        ts(T["shx" + n][:], T["ti" + n][:], 6, ALU.arith_shift_right, tab(k), ["shx" + n])
+        ti, x, k = T["ti" + n], T["xr" + n], tab("l" + n)
+        quarters = [slice(A * q, A * q + A) for q in range(4)]
+        for q in range(4):
+            ts(T.eqb[:, quarters[q]], T.dr[:], T.dcol[:, q:q + 1], ALU.is_equal, ["dr"] + dcol, ["eqb%d" % q])
+        scan(T.cum[:], T.rst[:], T.eqb[:], 0.0, ALU.mult, ALU.add, ["rst"] + ["eqb%d" % q for q in range(4)], ["cum"])
+        tt(T.xx[:], T.xm[:], T["xa" + n][:], ALU.add, ["xm", "xa" + n], ["xx"])
+        ts(T.cum[:], T.cum[:], T.r1[:, 0:1], ALU.is_lt, ["cum", "r1"], ["cum"], float(BIG), ALU.mult)
+        for q in range(4):
+            tt(T.yy[:, quarters[q]], T.cum[:, quarters[q]], T.xx[:], ALU.add, ["cum", "xx"], ["yy%d" % q])
+        scan(T.mn[:], T.rs2[:], T.yy[:], 0.0, ALU.max, ALU.min, ["rs2"] + ["yy%d" % q for q in range(4)], ["mn"])
+        for a in range(2):
+            for b in range(2):
+                cp(ti[64 * b:64 * b + 64, 4 * a:4 * a + 4], T.mn[64 * a:64 * a + 64, 31:128:32], ["mn"], ["tabl%s%d%d" % (n, a, b)])
+        send("xr" + n, lambda d: ti[:, place(d):place(d) + 1], lambda d: x[:, 4 * seen(d):4 * seen(d) + 1], k)
+        ts(T.shx[:], ti[:], 6, ALU.logical_shift_right, k, ["shx"], 255, ALU.bitwise_and)
+
+    def inverse(t):
+        n = str(t)
+        ts(T.ia[:], T["ti" + n][:], 14, ALU.logical_shift_right, tab("l" + n), ["ia"])
+        cp(T.so[:, 0:A], T.ioj[:], ["ioj"], ["so"])
+        ts(T.fl[:], T.ia[:], 32.0, ALU.is_ge, ["ia"], ["fl"])
+        tt(T.fl[:], T.fl[:], T.slott[:], ALU.mult, ["fl", "slott"], ["fl"])
+        tt(T.fl[:], T.fl[:], T.ia[:], ALU.add, ["fl", "ia"], ["fl"])
+        cp(T.lu[:], T.fl[:], ["fl"], ["lu"])
+        cp(T.so[:, 0:160].indirect(T.lu[:, 0:8]), T.rowc[:], ["rowc", "lu"], ["so"])
+        tt(T.dn[:], T.so[:, 0:A], T.mm[:, 0:A], ALU.mult, ["so", "mm"], ["dn"])
+        for h in range(2):
+            red(T.n2[:, h:h + 1], T.dn[:, 16 * h:16 * h + 16], ["dn"], ["n2%d" % h])
+        cp(T["nu" + n][:], T.n2[:], ["n20", "n21"], ["nu" + n])
 
     def received(t):
         n = str(t)
         xv = T["xr" + n][:, 0:4 * N:4]
         src = ["in_xr" + n, "xrown" + n]
         if t == 0:
-            ts(T.lsh[:], xv, 6, ALU.arith_shift_right, src, ["lsh"])
+            ts(T.ia[:], xv, 6, ALU.logical_shift_right, src, ["ia"], 255, ALU.bitwise_and)
         ts(T.vi[:], xv, 63, ALU.bitwise_and, src, ["vi"])
         if t == 0:
-            tt(T.lsa[:], T.lsh[:], T.fs[:], ALU.mult, ["lsh", "fs"], ["lsa"])
+            tt(T.fl[:], T.ia[:], T.fs[:], ALU.mult, ["ia", "fs"], ["fl"])
         tt(T.vm[:], T.vi[:], T.blk[:], ALU.mult, ["vi", "blk"], ["vm"])
         if t == 0:
-            tt(T.lsa[:], T.lsa[:], T.cc[:], ALU.add, ["lsa", "cc"], ["lsa"])
+            tt(T.fl[:], T.fl[:], T.cc[:], ALU.add, ["fl"] + ccs, ["fl"])
         red(T.v[:], T.vm[:], ["vm"], ["v"])
         if t == 0:
-            cp(T.lsu[:], T.lsa[:], ["lsa"], ["lsu"])
-        ts(T.zlf[:], T.ibq[:], T.v[:, 0:1], ALU.add, ["ibq", "v"], ["zlf"], 4.0, ALU.mult)
-        ts(T.ll[:, 3:4], T.v[:], 4.0, ALU.mult, ["v"], ["llz"])
-        cp(T["zl" + n][:], T.zlf[:], ["zlf"], ["zl" + n])
-        if t == 0:
+            cp(T.lsu[:], T.fl[:], ["fl"], ["lsu"])
             pick("land0", 0, "lx0", 256, T.lsu[:, 0:8], 128, ["in_lx0", "lx0own", "lx0own2", "lsu"], "land0")
-        tt(T.ng[:], T.nxf[:, 0:P].indirect(T["zl" + n][:, 0:4]), T.mm[:], ALU.mult, ["nxf", "zl" + n, "mm"], ["ng"])
-        for b in range(4):
-            red(T.n4[:, b:b + 1], T.ng[:, 16 * b:16 * b + 16], ["ng"], ["n4%d" % b])
-        n4 = ["n4%d" % b for b in range(4)]
-        tt(T.dn[:], T.n4[:, 1:4], T.n4[:, 0:3], ALU.subtract, n4, ["dn"])
-        cp(T.npr[:, 3:4], T.n4[:, 0:1], n4, ["npz"])
+        ts(T.zlf[:], T.ibq[:], T.v[:, 0:1], ALU.add, ["ibq", "v"], ["zlf"], 4.0, ALU.mult)
+        ts(T.v4[:], T.vi[:], 4.0, ALU.mult, ["vi"], ["v4"])
+        cp(T.zl[:], T.zlf[:], ["zlf"], ["zl"])
+
+    def goes(d):
+        return slice(CAPP * place(d), CAPP * place(d) + CAPP)
 
     def serve(t):
         n = str(t)
-        land, nt = "land" + n, T["nt" + n]
-        lk = ["land0_c", "land0_s"] if t == 0 else ["in_land1", "land1own", "land1own2"]
-        mx(0, P, land, 0, "kq", 0, lk + ["kq"])
+        land, nt, kp, xq, win = "land" + n, T["nt" + n], "kp" + n, "xq" + n, ("wina", "winb")[t]
+        lk = ["land0_c", "land0_s"] if t == 0 else ["in_land1", "land1own_c", "land1own_s"]
+        mx(0, 128, land, 0, "kq", 0, lk + ["kq"])
+        mx(5, 128, land, 0, "kq", 128, lk + ["kq"])
         for i in range(4):
-            mx(1 + i, 128, "h", 128 * i, land, 0, lk + ["h%d" % i])
-        act(T.zs[:], bank(0, P), ["bank0"], ["zs"])
+            mx(1 + i, 128, "h", 128 * i, land, 0, lk + ["h%d" % i], True, False)
+        act(T.zs[:, 0:128], bank(0, 128), ["bank0"], ["zs0"])
+        cp(T.zs[:, 128:256], bank(5, 128), ["bank5"], ["zs1"])
+        tt(T.zg[:], T.zs[:, 0:P].indirect(T.zl[:, 0:4]), T.dm[:], ALU.add, ["zs0", "zs1", "zl", "dm"], ["zg"])
+        scan(T.rm[:], T.zg[:], T.zg[:], -2e29, ALU.max, ALU.max, ["zg"], ["rm"])
+        for k in range(3):
+            ts(T.xb[:, k:4 * N:4], T.bki[:], T.rm[:, 16 * k + 15:16 * k + 16], ALU.add, ["bki", "rm", "xbz"], ["xb%d" % k], T.rm[:, 63:64], ALU.is_lt)
+        quant(xq, 0, 128, T.xb[:], ["xbz", "xb0", "xb1", "xb2"], [xq])
+        mx(6, 128, "ws", 0, xq, 0, ["ws", xq])
+        tt(T.fl[:], bank(6, N), T.v4[:], ALU.add, ["bank6", "v4"], ["fl"])
+        cp(T.ct[:], T.fl[:], ["fl"], ["ct"])
+        pick(kp, 0, "kq", P, T.ct[:, 0:8], 128, ["kq", "ct"], kp)
         for i in range(4):
-            act(T.dq[:, 128 * i:128 * i + 128], bank(1 + i, 128), ["bank%d" % (1 + i)], ["dq%d" % i])
-        tt(T.zg[:], T.zs[:, 0:P].indirect(T["zl" + n][:, 0:4]), T.dm[:], ALU.add, ["zs", "zl" + n, "dm"], ["zg"])
-        op("v", lambda e: e.tensor_tensor_scan(T.rm[:], T.zg[:], T.zg[:], -2e29, ALU.max, ALU.max), ["zg"], ["rm"])
-        ts(T.ll[:, 0:3], T.rm[:, 15:48:16], T.rm[:, 63:64], ALU.is_lt, ["rm"], ["ll"])
-        red(T.c[:], T.ll[:], ["ll", "llz"], ["c"])
-        tt(T.npr[:, 0:3], T.ll[:, 0:3], T.dn[:], ALU.mult, ["ll", "dn"], ["npr"])
-        k = "s" + n
-        steps = to_table(k, T.c, T.ct, "c")
-        next(steps)
-        red(T["node" + n][:], T.npr[:], ["npr", "npz"], ["node" + n])
-        next(steps)
-        send("rn" + n, lambda d: T["node" + n][:], lambda d: T["rn" + n][:, rank:rank + 1], ["node" + n])
-        dma("s", "rnown" + n, T["rn" + n][:, rank:rank + 1], T["node" + n][:], ["node" + n], ["rnown" + n])
+            mx(1 + i, 128, "h", 128 * i, kp, 0, [kp + "_c", kp + "_s", "h%d" % i], False, True)
+        nodt, rn = T["nodt" + n], T["rn" + n]
+        yk = ["yy0", "yy1", "yy2", "yy3"]
+        tt(T.yy[:], T.nxf[:, 0:P].indirect(T.ct[:, 0:8]), T.locrow[:], ALU.add, ["nxf", "ct", "locrow"], yk)
+        turn(nodt[:], T.yy[:], yk, ["nodt" + n])
+        send("rn" + n, lambda d: nodt[:, 32 * (d // 2):32 * (d // 2) + 1], lambda d: rn[:, 4 * rank:4 * rank + 1], ["nodt" + n])
         for i in range(4):
-            tt(nt[:, i:512:4], T.hk[:, P * i:P * i + P].indirect(T.ct[:, 0:8]), T.dq[:, 128 * i:128 * i + 128], ALU.add,
-               ["hk%d" % i, "dq%d" % i] + tab(k), ["nt%s%d" % (n, i)])
+            if i % 2:
+                act(nt[:, i:512:4], bank(1 + i, 128), ["bank%d" % (1 + i)], ["nt%s%d" % (n, i)])
+            else:
+                cp(nt[:, i:512:4], bank(1 + i, 128), ["bank%d" % (1 + i)], ["nt%s%d" % (n, i)])
         quant("new" + n, 0, 128, nt[:], ["nt%s%d" % (n, i) for i in range(4)], ["new" + n])
-        win, at = ("wina", 128) if t == 0 else ("winb", A)
-        at += CAPP * rank
-        send("ret%s_c" % n, lambda d: codes("new" + n, CAPP * d, CAPP * d + CAPP), lambda d: codes(win, at, at + CAPP), ["new" + n])
-        send("ret%s_s" % n, lambda d: T["new%ss" % n][:, CAPP * d:CAPP * d + CAPP], lambda d: T[win + "s"][:, at:at + CAPP], ["new" + n])
-        dma("a", "self" + n, codes(win, at, at + CAPP), codes("new" + n, CAPP * rank, CAPP * rank + CAPP), ["new" + n], [win + "own"])
-        dma("a", "self" + n, T[win + "s"][:, at:at + CAPP], T["new%ss" % n][:, CAPP * rank:CAPP * rank + CAPP], ["new" + n], [win + "own2"])
-        dma("s", "row" + n, T["row" + n][0:1, :], T["rn" + n][CAPP * rank:CAPP * rank + CAPP, 0:N], ["in_rn" + n, "rnown" + n], ["row" + n])
-        op("g", lambda e: e.partition_broadcast(T["mrs" + n][:, A:A + 128], T["row" + n][0:1, :], 128), ["row" + n], ["mrsr" + n])
 
-    def slotmap(t):
+        def back(d):
+            return A + CAPP * seen(d)
+
+        send("ret%s_c" % n, lambda d: codes("new" + n, CAPP * place(d), CAPP * place(d) + CAPP), lambda d: codes(win, back(d), back(d) + CAPP), ["new" + n])
+        send("ret%s_s" % n, lambda d: T["new%ss" % n][:, goes(d)], lambda d: T[win + "s"][:, back(d):back(d) + CAPP], ["new" + n])
+        cp(rn[:, 4 * rank:4 * rank + 1], nodt[:, 32 * (rank // 2):32 * (rank // 2) + 1], ["nodt" + n], ["rnown" + n])
+        pick(win, back(rank), "new" + n, 128, T.ol[:, 0:1], CAPP, ["new" + n, "ol"], win + "own")
+
+    def home(t):
         n = str(t)
-        dr = T["dr" + n]
-        for d in range(N):
-            ts(T.e8[:, A * d:A * d + A], dr[:], float(d), ALU.is_equal, ["dr" + n], ["e8%d" % d])
-        e8 = ["e8%d" % d for d in range(N)]
-        op("v", lambda e: e.tensor_tensor_scan(T.c8[:], T.rst[:], T.e8[:], 0.0, ALU.mult, ALU.add), e8 + ["rst"], ["c8"])
-        base = 128 if t == 0 else A
-        ts(T.ta[:], dr[:], 16.0, ALU.mult, ["dr" + n], ["ta"], float(base - 1), ALU.add)
-        tt(T.c8[:], T.c8[:], T.e8[:], ALU.mult, e8 + ["c8"], ["c8"])
-        tt(T.nb[:], dr[:], T.af[:], ALU.subtract, ["dr" + n, "af"], ["nb"])
-        tt(T.c8[:, 0:128], T.c8[:, 0:128], T.c8[:, 128:256], ALU.add, ["c8"], ["c8"])
-        tt(T.c8[:, 0:64], T.c8[:, 0:64], T.c8[:, 64:128], ALU.add, ["c8"], ["c8"])
-        tt(T.rk[:], T.c8[:, 0:32], T.c8[:, 32:64], ALU.add, ["c8"], ["rk"])
-        ts(T.sv[:], T.rk[:], float(CAPP), ALU.is_le, ["rk"], ["sv"])
-        ts(T.na[:], T.rk[:], 8.0, ALU.mult, ["rk"], ["na"], float(A - 8), ALU.add)
-        tt(T.tb[:], T.rk[:], T.af[:], ALU.subtract, ["rk", "af"], ["tb"])
-        tt(T.na[:], T.na[:], T.nb[:], ALU.add, ["na", "nb"], ["na"])
-        tt(T.ta[:], T.ta[:], T.tb[:], ALU.add, ["ta", "tb"], ["ta"])
-        tt(T.na[:], T.na[:], T.sv[:], ALU.mult, ["na", "sv"], ["na"])
-        tt(T.ta[:], T.ta[:], T.sv[:], ALU.mult, ["ta", "sv"], ["ta"])
-        tt(T.na[:], T.na[:], T.af[:], ALU.add, ["na", "af"], ["na"])
-        tt(T.ta[:], T.ta[:], T.af[:], ALU.add, ["ta", "af"], ["ta"])
-        tt(T.nb[:], T.na[:], T.mm[:, 0:A], ALU.mult, ["na", "mm"], ["nb"])
-        tt(T.tb[:], T.ta[:], T.mm[:, 0:A], ALU.mult, ["ta", "mm"], ["tb"])
-        for h in range(2):
-            red(T.n2[:, h:h + 1], T.nb[:, 16 * h:16 * h + 16], ["nb"], ["n2%d" % h])
-            red(T.l2[:, h:h + 1], T.tb[:, 16 * h:16 * h + 16], ["tb"], ["l2%d" % h])
-        if t == 0:
-            ts(T.loc641[:], T.ta[:], 64.0, ALU.mult, ["ta"], ["loc641"])
-        cp(T["nu" + n][:], T.n2[:], ["n20", "n21"], ["nu" + n])
-        cp(T["lu" + n][:], T.l2[:], ["l20", "l21"], ["lu" + n])
+        vv = T["vv" + n]
+        cp(T.vm[:], T["rn" + n][:, 0:4 * N:4], ["in_rn" + n, "rnown" + n], ["vm"])
+        cp(T.mn[:], T.vm[:, 0:N].indirect(T.elst[:, 0:8]), ["vm", "elst"], ["mn"])
+        turn(T.win[:, A:160], T.mn[:], ["mn"], ["winr"])
+        cp(vv[:], T.win[:, 0:160].indirect(T["nu" + n][:, 0:2]), ["winq", "winr", "nu" + n], ["vv" + n])
+        ts(T.dr[:], vv[:], 14, ALU.logical_shift_right, ["vv" + n], ["dr"])
 
-    cp(T.nri0[:, 0:16], T.strb[:, 0:A:2], ["strb"], ["nri0"])
-    cp(T.nri0[:, 16:32], T.strb[:, 1:A:2], ["strb"], ["nri0"])
+    def number(t):
+        n = str(t)
+        ts(T.dl[:], T["vv" + n][:], 63, ALU.bitwise_and, ["vv" + n], ["dl"])
+        ts(T.dn[:], T.dr[:], 64.0, ALU.mult, ["dr"], ["dn"])
+        tt(T["ndf" + n][:], T.dn[:], T.dl[:], ALU.add, ["dl", "dn"], ["ndf" + n])
+
+    for h in range(2):
+        ts(T.dr[:, 16 * h:16 * h + 16], T.strb[:, h:A:2], 6, ALU.arith_shift_right, ["strb"], ["dr"])
+    for h in range(2):
+        ts(T.xm[:, 16 * h:16 * h + 16], T.strb[:, h:A:2], 63, ALU.bitwise_and, ["strb"], ["xm"])
     lists(0)
     for i, c in enumerate(picked):
-        d = cores.index(c)
-        cp(T.pl[:, i:i + 1], T.shx0[:, d:d + 1], ["shx0"], ["pl%d" % i])
+        k = place(cores.index(c))
+        cp(T.pl[:, i:i + 1], T.shx[:, k:k + 1], ["shx"], ["pl%d" % i])
     pick("send0", 0, "qx", 128, T.pl[:, 0:2], 32, ["qx", "pl0", "pl1"], "send0")
     slot = {cores.index(c): i * CAPP for i, c in enumerate(picked)}
-    send("pick_c", lambda d: codes("send0", slot[d], slot[d] + CAPP), lambda d: codes("lx0", A * rank, A * rank + CAPP), ["send0_c"])
-    send("pick_s", lambda d: T.send0s[:, slot[d]:slot[d] + CAPP], lambda d: T.lx0s[:, A * rank:A * rank + CAPP], ["send0_s"])
-    cp(T.xr0[:, 4 * rank:4 * rank + 1], T.ti0[:, rank:rank + 1], tab("l0"), ["xrown0"])
-    op("g", lambda e: e.partition_broadcast(T.nxr[:], T.nx1[0:1, :], 128), ["nx1"], ["nxr"])
+    send("pick_c", lambda d: codes("send0", slot[d], slot[d] + CAPP), lambda d: codes("lx0", A * seen(d), A * seen(d) + CAPP), ["send0_c"])
+    send("pick_s", lambda d: T.send0s[:, slot[d]:slot[d] + CAPP], lambda d: T.lx0s[:, A * seen(d):A * seen(d) + CAPP], ["send0_s"])
+    cp(T.xr0[:, 4 * me:4 * me + 1], T.ti0[:, me:me + 1], tab("l0"), ["xrown0"])
+    ts(T.nxh[0:32, :], T.nxt[0:32, :], 6, ALU.arith_shift_right, ["nxt"], ["nxh"])
+    ts(T.nxp[0:32, :], T.nxh[0:32, :], float(16384 - 64), ALU.mult, ["nxh"], ["nxp"])
+    tt(T.nxp[0:32, :], T.nxp[0:32, :], T.nxt[0:32, :], ALU.add, ["nxp", "nxt"], ["nxp"])
+    turn(T.nxq[0:32, :], T.nxp[0:32, :], ["nxp"], ["nxq"])
+    dma("s", "nxr", T.nx1[0:1, :], T.nxq[0:16, 0:16], ["nxq"], ["nx1"])
+    for k in range(3):
+        act(T.wb[:, k:512:4], T.mm[:], ["mm", "wb"], ["wb%d" % k])
+    ts(T.pd[:], T.iop[:], 4, ALU.arith_shift_right, ["iop"], ["pd"])
+    fill(T.fs[:], 1.0, ["fs"])
+    ts(T.cc[:], T.ioj[:, 0:N], 32.0, ALU.mult, ["ioj"], ["cc"])
+    tt(T.blk[:], T.pd[:], T.ioj[:, 0:N], ALU.is_equal, ["pd", "ioj"], ["blk"])
+    ccs = ["cc"]
+    for s, c in enumerate(cores):
+        if c != core and core in plans[c][1]:
+            k = place(s)
+            fill(T.fs[:, k:k + 1], 0.0, ["fs"])
+            ts(T.cc[:, k:k + 1], T.r1[:], float(32 * k - 1), ALU.add, ["r1", "cc"], ["cc%d" % k])
+            ccs.append("cc%d" % k)
+    ts(T.ibq[:], T.ioj[:, 0:4], 0.25, ALU.mult, ["ioj"], ["ibq"])
     quant("kq", 0, P, T.kt[:], ["kt"], ["kq"])
     for i in range(4):
         quant("h", 128 * i, 128 * i + 128, T.hb[:, 3 - i:515 - i], ["hb"], ["h%d" % i])
-        mx(1 + i, P, "h", 128 * i, "kq", 0, ["kq", "h%d" % i])
-        act(T.hk[:, P * i:P * i + P], bank(1 + i, P), ["bank%d" % (1 + i)], ["hk%d" % i])
-    ts(T.j15[:, 0:16], T.p15[:, 0:16], 16.0, ALU.mult, ["p15"], ["j15"])
-    tt(T.j15[:, 0:16], T.j15[:, 0:16], T.ioj[:, 0:16], ALU.add, ["j15", "ioj"], ["j15"])
-    cp(T.pi[:], T.j15[:, 0:16], ["j15"], ["pi"])
-    cp(T.nxf[:], T.nxr[:, 0:P].indirect(T.pi[:, 0:16]), ["nxr", "pi"], ["nxf"])
+    ts(T.bki[:], T.blk[:], -1.0, ALU.add, ["blk"], ["bki"], -1e29, ALU.mult)
+    ts(T.dm[:], T.mm[:, 0:64], -1.0, ALU.add, ["mm"], ["dm"], 1e29, ALU.mult)
+    quant("ws", 0, 128, T.wb[:], ["wb", "wb0", "wb1", "wb2"], ["ws"])
+    op("g", lambda e: e.partition_broadcast(T.nxf[:], T.nx1[0:1, :], 128), ["nx1"], ["nxf"])
+    iota(T.locrow[:], [[0, 4], [64, 32]], 64 * (A + 32 * (rank // 2)), 0, ["locrow"], True)
+    iota(T.el[:], [[2, 4], [0, 2]], 0, 0, ["el"])
+    iota(T.rowc[:], [[1, 128]], A, 0, ["rowc"], True)
+    iota(T.io16[:], [[16, 8]], -1, 0, ["io16"])
+    iota(T.xa1[:], [[16384, A]], 0, 0, ["xa1"], True)
     received(0)
+    ts(T.ol[:, 0:1], T.r1[:], float(mine - 1), ALU.add, ["r1"], ["ol"])
     serve(0)
-    fill(T.rst[:], 1.0, ["rst"])
-    fill(T.rst[:, 0:256:32], 0.0, ["rst"])
-    cp(T.af[:], T.ioj[:, 0:A], ["ioj"], ["af"])
-    cp(T.mrs0[:, 0:A], T.nri0[:], ["nri0"], ["mrsq0"])
-    slotmap(0)
-    quant("wina", 0, 128, T.xt[:], ["xt", "xtz"], ["winaq"])
-    cp(T.nri1[:], T.mrs0[:, 0:160].indirect(T.nu0[:, 0:2]), ["mrsq0", "mrsr0", "nu0"], ["nri1"])
+    dma("s", "w", T.wt[:], T.w[:], [], ["wt"])
+    dma("s", "ownw", codes("wina", 0, A), codes("qx", 0, A), ["qx"], ["winaq"])
+    dma("s", "ownw", T.winas[:, 0:A], T.qxs[:, 0:A], ["qx"], ["winaq2"])
+    ts(T.win[:, 0:A], T.dr[:], 16384.0, ALU.mult, ["dr"], ["winq"])
+    ts(T.slott[:], T.io16[:], T.r1[:, 0:1], ALU.add, ["io16", "r1"], ["slott"])
+    ts(T.ia[:], T.pd[:], 1, ALU.bitwise_and, ["pd"], ["ia"])
+    tt(T.win[:, 0:A], T.win[:, 0:A], T.xx[:], ALU.add, ["winq", "xx"], ["winq"])
+    ts(T.fl[:], T.ia[:], -1.0 if odd else 1.0, ALU.mult, ["ia"], ["fl"], float(odd), ALU.add)
+    tt(T.win[:, 0:A], T.win[:, 0:A], T.xa1[:], ALU.subtract, ["winq", "xa1"], ["winq"])
+    tt(T.fl[:], T.fl[:], T.el[:], ALU.add, ["fl", "el"], ["fl"])
+    cp(T.elst[:], T.fl[:], ["fl"], ["elst"])
+    inverse(0)
+    home(0)
+    ts(T.xm[:], T.vv0[:], 16383, ALU.bitwise_and, ["vv0"], ["xm"])
     lists(1)
-    cp(T.sl[:], T.shx1[:], ["shx1"], ["sl"])
-    cp(T.xr1[:, 4 * rank:4 * rank + 1], T.ti1[:, rank:rank + 1], tab("l1"), ["xrown1"])
-    wina = ["winaq", "winaown", "winaown2", "in_ret0"]
-    pick("send1", 0, "wina", 256, T.sl[:, 0:8], 128, wina + ["sl"], "send1")
-    at = CAPP * rank
-    send("land1_c", lambda d: codes("send1", CAPP * d, CAPP * d + CAPP), lambda d: codes("land1", at, at + CAPP), ["send1_c"])
-    send("land1_s", lambda d: T.send1s[:, CAPP * d:CAPP * d + CAPP], lambda d: T.land1s[:, at:at + CAPP], ["send1_s"])
-    dma("s", "own1", codes("land1", at, at + CAPP), codes("send1", at, at + CAPP), ["send1_c"], ["land1own"])
-    dma("s", "own1", T.land1s[:, at:at + CAPP], T.send1s[:, at:at + CAPP], ["send1_s"], ["land1own2"])
-    cp(T.mrs1[:, 0:A], T.nri1[:], ["nri1"], ["mrsq1"])
-    dma("s", "nd0", T.nd[0:1, :], T.mrs0[0:1, 0:A], ["mrsq0"], [])
-    dma("s", "nd1", T.nd[1:2, :], T.mrs1[0:1, 0:A], ["mrsq1"], [])
+    cp(T.sl[:], T.shx[:], ["shx"], ["sl"])
+    wina = ["winaq", "winaq2", "winaown_c", "winaown_s", "in_ret0"]
+    pick("send1", 0, "wina", 160, T.sl[:, 0:8], 128, wina + ["sl"], "send1")
+    send("land1_c", lambda d: codes("send1", CAPP * place(d), CAPP * place(d) + CAPP),
+         lambda d: codes("land1", CAPP * seen(d), CAPP * seen(d) + CAPP), ["send1_c"])
+    send("land1_s", lambda d: T.send1s[:, goes(d)], lambda d: T.land1s[:, CAPP * seen(d):CAPP * seen(d) + CAPP], ["send1_s"])
+    cp(T.xr1[:, 4 * me:4 * me + 1], T.ti1[:, me:me + 1], tab("l1"), ["xrown1"])
+    pick("land1", mine, "send1", 128, T.ol[:, 0:1], CAPP, ["send1_c", "send1_s", "ol"], "land1own")
+    for h in range(2):
+        cp(T.nd0f[:, 16 * h:16 * h + 16], T.strb[:, h:A:2], ["strb"], ["nd0f"])
+    number(0)
     received(1)
     serve(1)
-    slotmap(1)
-    pick("winb", 0, "wina", 256, T.lu0[:, 0:2], A, wina + ["lu0"], "winbq")
+    dma("s", "nd0", T.nd[0:1, :], T.nd0f[0:1, :], ["nd0f"], [])
+    dma("s", "nd1", T.nd[1:2, :], T.ndf0[0:1, :], ["ndf0"], [])
+    cp(T.win[:, 0:A], T.vv0[:], ["vv0"], ["winq"])
+    inverse(1)
+    pick("winb", 0, "wina", 160, T.nu0[:, 0:2], A, wina + ["nu0"], "winbq")
     quant("wq", 0, 128, T.wt[:], ["wt"], ["wq"])
     quant("fin", 0, 128, T.xt[:], ["xt", "xtz"], ["fin_c", "fin_s"])
-    pick("fin", 0, "winb", 160, T.lu1[:, 0:2], A, ["winbq_c", "winbq_s", "winbown", "winbown2", "in_ret1", "lu1"], "fin")
-    mx(5, 128, "wq", 0, "fin", 0, ["wq", "fin_c", "fin_s"])
-    act(T.ys[:], bank(5, A), ["bank5"], ["ys"])
+    home(1)
+    number(1)
+    dma("s", "nd2", T.nd[2:3, :], T.ndf1[0:1, :], ["ndf1"], [])
+    pick("fin", 0, "winb", 160, T.nu1[:, 0:2], A, ["winbq_c", "winbq_s", "winbown_c", "winbown_s", "in_ret1", "nu1"], "fin")
+    mx(7, 128, "wq", 0, "fin", 0, ["wq", "fin_c", "fin_s"])
+    act(T.ys[:], bank(7, A), ["bank7"], ["ys"])
     dma("a", "y", T.y[:], T.ys[:], ["ys"], [])
     dma("s", "oc", T.oc[:], codes("fin", 0, A), ["fin_c"], [])
     for k in range(4):
         dma("s" if k % 2 else "a", "osc", T.osc[4 * k:4 * k + 4, :], T.fins[32 * k:32 * k + 4, 0:A], ["fin_s"], [])
-    cp(T.nr2[:], T.mrs1[:, 0:160].indirect(T.nu1[:, 0:2]), ["mrsq1", "mrsr1", "nu1"], ["nr2"])
-    dma("s", "nd2", T.nd[2:3, :], T.nr2[0:1, :], ["nr2"], [])
     g.wait_ge(T.sem.left, left[0])
     for q, s in sems.items():
         g.wait_ge(T.sem[s], count[q])

from concourse.bass import DstId, RemoteDMATransfer
from concourse.mybir import dt, AluOpType, AxisListType, ActivationFunctionType

N, P, A, CAPP = 8, 256, 32, 16
F8, U8, F32, BF, I32, U16 = "float8_e4m3fn_x4", "uint8", "float32", "bfloat16", "int32", "uint16"
BIG = 32 * 16384
SCRATCH = {}


def _add(name, cols, dtype, where="sbuf"):
    SCRATCH[name] = (where, [128, cols], dtype)


for _n, _c in (("qx", 128), ("lx0", 256), ("send0", 32), ("land0", 128), ("new0", 128), ("wina", 160), ("send1", 128),
               ("land1", 128), ("new1", 128), ("winb", 160), ("fin", 128), ("kq", 256), ("wq", 128), ("h", 512), ("ws", 128),
               ("kp0", 128), ("kp1", 128), ("xq0", 128), ("xq1", 128)):
    _add(_n + "c", _c, F8)
    _add(_n + "s", _c, U8)
for _n, _c, _d in (("xt", 512, BF), ("kt", 1024, BF), ("wt", 512, BF), ("hb", 516, BF), ("wb", 512, BF), ("xb", 512, BF),
                   ("iop", 8, I32), ("ioj", 32, I32), ("jmp", 128, I32), ("xa0", 32, F32), ("xa1", 32, F32),
                   ("el", 8, I32), ("elst", 8, U16), ("locrow", 128, F32), ("rowc", 128, F32), ("io16", 8, I32), ("slott", 8, F32),
                   ("pd", 8, I32), ("mm", 128, F32), ("dm", 64, F32), ("blk", 8, F32), ("bki", 8, F32),
                   ("r1", 1, F32), ("ibq", 4, F32), ("dcol", 4, F32), ("rst", 128, BF), ("rs2", 128, F32),
                   ("fs", 8, F32), ("cc", 8, F32), ("str1", 32, I32), ("strb", 32, I32), ("nd0f", 32, F32),
                   ("nxt", 32, I32), ("nxh", 32, I32), ("nxp", 32, F32), ("nxq", 32, F32), ("nx1", 256, F32), ("nxf", 256, F32),
                   ("lsu", 8, U16), ("pl", 2, U16), ("sl", 8, U16), ("ol", 2, U16), ("ys", 32, F32),
                   ("dr", 32, I32), ("xm", 32, I32), ("xx", 32, F32), ("shx", 8, I32), ("zl", 4, U16), ("ct", 8, U16),
                   ("win", 160, F32), ("lu", 8, U16), ("so", 160, F32), ("dn", 32, F32), ("dl", 32, I32),
                   ("vi", 8, I32), ("vm", 8, F32), ("v", 1, F32), ("v4", 8, F32), ("zlf", 4, F32), ("zs", 256, F32), ("zg", 64, F32), ("rm", 64, F32),
                   ("eqb", 128, BF), ("cum", 128, BF), ("yy", 128, F32), ("mn", 128, F32),
                   ("ia", 8, I32), ("fl", 8, F32), ("n2", 2, F32)):
    _add(_n, _c, _d)
for _t in ("0", "1"):
    for _n, _c, _d in (("ti", 8, I32), ("xr", 32, I32), ("nodt", 128, F32), ("nt", 512, BF), ("rn", 32, F32),
                       ("vv", 32, I32), ("nu", 2, U16), ("ndf", 32, F32)):
        _add(_n + _t, _c, _d)
_add("bank", 512 * 8, F32, "psum")
ARRIVE = ["lx0", "xr0", "rn0", "ret0", "xr1", "land1", "rn1", "ret1"]
DMAS = ["st", "x", "ky", "nx", "w", "nxr", "own0", "ownw", "nd0", "nd1", "nd2", "oc", "osc", "y"]
SEMAPHORES = ["sg", "sv", "sa", "sp", "left"] + ["a_" + k for k in ARRIVE] + ["d_" + k for k in DMAS]


def _bits(m):
    return bin(m).count("1")


def _plan(topo, cores, me):
    others = [c for c in cores if c != me]
    near = [c for c in others if c in topo.cores_of(me)]
    far = [c for c in others if c not in near]
    mate = [c for c in far if topo.mates(me, c) and topo.die(me) == topo.die(c)]
    port = topo.engines(me, far[0])
    rest = [e for e in topo.engines(me, near[0]) if e not in port]
    load = {e: 0 for e in port}
    turn = [0]

    def masks(dsts):
        o = {}
        for c in dsts:
            if c in near:
                o[c] = sum(1 << e for e in rest)
        f = [c for c in dsts if c in far]
        if len(f) == 1:
            o[f[0]] = sum(1 << e for e in port)
            return o
        k = turn[0] % len(f)
        turn[0] += 2
        f = f[k:] + f[:k]
        free = sorted(port, key=lambda e: load[e])
        doubles = len(free) - len(f)
        for i, c in enumerate(f):
            take = 1 if i < len(f) - doubles else 2
            o[c] = sum(1 << e for e in free[:take])
            for e in free[:take]:
                load[e] += 2 // take
            free = free[take:]
        return o

    picked = near + mate
    wide = [c for c in far if c not in picked]
    out = {"wide_c": masks(wide), "wide_s": masks(wide), "xr0": masks(others), "pick_c": masks(picked), "pick_s": masks(picked)}
    for k in ("rn0", "ret0_c", "ret0_s", "xr1", "land1_c", "land1_s", "rn1", "ret1_c", "ret1_s"):
        out[k] = masks(others)
    return out, picked, wide


ROUTE = {"wide_c": "lx0", "wide_s": "lx0", "pick_c": "lx0", "pick_s": "lx0", "xr0": "xr0", "rn0": "rn0", "ret0_c": "ret0", "ret0_s": "ret0",
         "xr1": "xr1", "land1_c": "land1", "land1_s": "land1", "rn1": "rn1", "ret1_c": "ret1", "ret1_s": "ret1"}


def rank_program(g, core, T, topo):
    rank = T.rank_of(core)
    if rank is None:
        return
    cores = list(T.cores)
    odd = rank % 2
    plans = {c: _plan(topo, cores, c) for c in cores}
    calls, picked, wide = plans[core]
    want = {k: 0 for k in ARRIVE}
    for c in cores:
        if c != core:
            for k, a in ROUTE.items():
                want[a] += _bits(plans[c][0][k].get(core, 0))
    ALU, X, CP = AluOpType, AxisListType.X, ActivationFunctionType.Copy
    queues = {"g": g, "v": g.vector, "a": g.scalar, "p": g.tensor, "s": g.sync}
    sems = {"g": "sg", "v": "sv", "a": "sa", "p": "sp"}
    count = {k: 0 for k in sems}
    known = {k: {} for k in queues}
    snap = {}
    wrote, readers = {}, {}

    def waits(q, reads, writes):
        need = [wrote[k] for k in reads]
        for k in writes:
            if k in wrote:
                need.append(wrote[k])
            for e, rq in readers.get(k, []):
                if rq != q or e[0].startswith("d_"):
                    need.append(e)
        best = {}
        for s, val in need:
            if known[q].get(s, 0) < val:
                best[s] = max(best.get(s, 0), val)
        for s in sorted(best, key=lambda s: -len(snap.get((s, best[s]), {}))):
            val = best[s]
            if known[q].get(s, 0) >= val:
                continue
            queues[q].wait_ge(T.sem[s], val)
            known[q][s] = val
            for s2, v2 in snap.get((s, val), {}).items():
                known[q][s2] = max(known[q].get(s2, 0), v2)

    def note(q, ev, reads, writes):
        snap[ev] = dict(known[q])
        for k in reads:
            readers.setdefault(k, []).append((ev, q))
        for k in writes:
            wrote[k] = ev
            readers[k] = []

    def op(q, fn, reads, writes):
        waits(q, reads, writes)
        count[q] += 1
        fn(queues[q]).then_inc(T.sem[sems[q]], 1)
        note(q, (sems[q], count[q]), reads, writes)

    dcount = {}

    def dma(q, name, out, in_, reads, writes):
        s = "d_" + name
        waits(q, reads, writes)
        queues[q].dma_start(out, in_).then_inc(T.sem[s], 16)
        dcount[s] = dcount.get(s, 0) + 16
        note(q, (s, dcount[s]), reads, writes)

    left = [0]

    def send(call, src, dst, reads):
        waits("g", reads, [])
        tr = []
        for c, m in calls[call].items():
            rid, pid = topo.addr(c, core)
            d = cores.index(c)
            tr.append(RemoteDMATransfer(dst_ids=[DstId(rid=rid, pnc=pid)], dma_engine_mask=m, remote_sem=T.sem["a_" + ROUTE[call]], src=src(d), dst=dst(d)))
            left[0] += _bits(m)
        g.remote_dma_fused(tr, local_sem=T.sem.left)

    for k in ARRIVE:
        wrote["in_" + k] = ("a_" + k, want[k])

    def codes(name, a, b):
        return T[name + "c"][:, a:b].bitcast(dt.uint8)

    def words(name, a, b):
        return T[name + "c"][:, a:b].bitcast(dt.uint32)

    def ts(out, in0, s1, op0, reads, writes, s2=None, op1=None):
        if op1 is None:
            op("v", lambda e: e.tensor_scalar(out, in0, s1, None, op0), reads, writes)
        else:
            op("v", lambda e: e.tensor_scalar(out, in0, s1, s2, op0, op1), reads, writes)

    def tt(out, a, b, o, reads, writes):
        op("v", lambda e: e.tensor_tensor(out, a, b, o), reads, writes)

    def cp(out, a, reads, writes):
        op("v", lambda e: e.tensor_copy(out, a), reads, writes)

    def red(out, a, reads, writes, o=ALU.add):
        op("v", lambda e: e.tensor_reduce(out, a, X, o), reads, writes)

    def scan(out, a, b, init, o0, o1, reads, writes):
        op("v", lambda e: e.tensor_tensor_scan(out, a, b, init, o0, o1), reads, writes)

    def turn(out, a, reads, writes):
        op("v", lambda e: e.transpose(out, a), reads, writes)

    def fill(ap, value, writes):
        op("v", lambda e: e.memset(ap, value), [], writes)

    def quant(name, a, b, tile, reads, writes):
        op("v", lambda e: e.quantize_mx(T[name + "c"][:, a:b], T[name + "s"][:, a:b], tile), reads, writes)

    def iota(out, pattern, base, step, writes, flag=False):
        if flag:
            op("g", lambda e: e.iota(out, pattern, base, step, allow_small_or_imprecise_dtypes=True), [], writes)
        else:
            op("g", lambda e: e.iota(out, pattern, base, step), [], writes)

    def mx(bank, n, l, la, r, ra, reads, start=True, stop=True):
        op("p", lambda e: e.matmul_mx(T.bank[:, 512 * bank:512 * bank + n], T[l + "c"][:, la:la + 128], T[l + "s"][:, la:la + 128],
                                      T[r + "c"][:, ra:ra + n], T[r + "s"][:, ra:ra + n], start, stop), reads, ["bank%d" % bank])

    def bank(k, n):
        return T.bank[:, 512 * k:512 * k + n]

    def act(out, in_, reads, writes):
        op("a", lambda e: e.activation(out, in_, CP), reads, writes)

    def zero(out, in_, reads, writes):
        op("a", lambda e: e.activation(out, in_, CP, scale=0.0), reads, writes)

    def pick(out, oa, win, wb, off, n, reads, key):
        cp(words(out, oa, oa + n), words(win, 0, wb).indirect(off), reads, [key + "_c"])
        act(T[out + "s"][:, oa:oa + n], T[win + "s"][:, 0:wb].indirect(off), reads, [key + "_s"])

    def place(r):
        return r ^ odd

    def seen(r):
        return rank ^ (r % 2)

    me = place(rank)
    mine = CAPP * me
    dma("s", "st", T.str1[0:1, 0:A], T.st[:], [], ["str1"])
    dma("a", "x", T.xt[:, 0:4 * A], T.x[:], [], ["xt"])
    dma("s", "ky", T.kt[:], T.ky[:], [], ["kt"])
    fill(T.nxt[0:32, :], 0, ["nxt"])
    iota(T.jmp[:], [[1, 128]], 0, -1, ["jmp"])
    iota(T.iop[:], [[0, 8]], 0, 1, ["iop"])
    iota(T.ioj[:], [[1, A]], 0, 0, ["ioj"])
    iota(T.xa0[:], [[16384 + 64, A]], 0, 0, ["xa0"], True)
    dma("a", "nx", T.nxt[0:16, 0:16], T.nx[:], ["nxt"], ["nxt"])
    fill(T.xt[:, 4 * A:512], 0.0, ["xtz"])
    fill(T.hb[:], 0.0, ["hb"])
    dcol = []
    for q in range(4):
        for half in range(2):
            dcol.append("dcol%d%d" % (q, half))
            fill(T.dcol[64 * half:64 * half + 64, q:q + 1], float(place(4 * half + q)), dcol[-1:])
    ts(T.hb[:, 3:515:4], T.jmp[:], 0.0, ALU.is_equal, ["jmp"], ["hb"], 0.5, ALU.mult)
    ts(T.ia[:], T.iop[:], 15, ALU.bitwise_and, ["iop"], ["ia"])
    fill(T.rst[:], 1.0, ["rst"])
    fill(T.rst[:, 0:128:32], 0.0, ["rst"])
    fill(T.rs2[:], 0.0, ["rs2"])
    fill(T.rs2[:, 0:128:32], float(4 * BIG), ["rs2"])
    ts(T.r1[:], T.ia[:, 0:1], 1.0, ALU.add, ["ia"], ["r1"])
    ts(T.jmp[:], T.jmp[:], 15, ALU.bitwise_and, ["jmp"], ["jmp"])
    ts(T.mm[:], T.jmp[:], 0.0, ALU.is_equal, ["jmp"], ["mm"])
    zero(T.xb[:], T.hb[:, 0:512], ["hb"], ["xbz"])
    zero(T.wb[:], T.hb[:, 0:512], ["hb"], ["wb"])
    quant("qx", 0, 128, T.xt[:], ["xt", "xtz"], ["qx"])
    op("g", lambda e: e.partition_broadcast(T.strb[:], T.str1[0:1, 0:A], 128), ["str1"], ["strb"])
    send("wide_c", lambda d: codes("qx", 0, A), lambda d: codes("lx0", A * seen(d), A * seen(d) + A), ["qx"])
    send("wide_s", lambda d: T.qxs[:, 0:A], lambda d: T.lx0s[:, A * seen(d):A * seen(d) + A], ["qx"])
    dma("s", "own0", codes("lx0", A * me, A * me + A), codes("qx", 0, A), ["qx"], ["lx0own"])
    dma("s", "own0", T.lx0s[:, A * me:A * me + A], T.qxs[:, 0:A], ["qx"], ["lx0own2"])

    def tab(k):
        return ["tab%s%d%d" % (k, a, b) for a in range(2) for b in range(2)]

    def lists(t):
        n = str(t)
        ti, x, k = T["ti" + n], T["xr" + n], tab("l" + n)
        quarters = [slice(A * q, A * q + A) for q in range(4)]
        for q in range(4):
            ts(T.eqb[:, quarters[q]], T.dr[:], T.dcol[:, q:q + 1], ALU.is_equal, ["dr"] + dcol, ["eqb%d" % q])
        scan(T.cum[:], T.rst[:], T.eqb[:], 0.0, ALU.mult, ALU.add, ["rst"] + ["eqb%d" % q for q in range(4)], ["cum"])
        tt(T.xx[:], T.xm[:], T["xa" + n][:], ALU.add, ["xm", "xa" + n], ["xx"])
        ts(T.cum[:], T.cum[:], T.r1[:, 0:1], ALU.is_lt, ["cum", "r1"], ["cum"], float(BIG), ALU.mult)
        for q in range(4):
            tt(T.yy[:, quarters[q]], T.cum[:, quarters[q]], T.xx[:], ALU.add, ["cum", "xx"], ["yy%d" % q])
        scan(T.mn[:], T.rs2[:], T.yy[:], 0.0, ALU.max, ALU.min, ["rs2"] + ["yy%d" % q for q in range(4)], ["mn"])
        for a in range(2):
            for b in range(2):
                cp(ti[64 * b:64 * b + 64, 4 * a:4 * a + 4], T.mn[64 * a:64 * a + 64, 31:128:32], ["mn"], ["tabl%s%d%d" % (n, a, b)])
        send("xr" + n, lambda d: ti[:, place(d):place(d) + 1], lambda d: x[:, 4 * seen(d):4 * seen(d) + 1], k)
        ts(T.shx[:], ti[:], 6, ALU.logical_shift_right, k, ["shx"], 255, ALU.bitwise_and)

    def inverse(t):
        n = str(t)
        ts(T.ia[:], T["ti" + n][:], 14, ALU.logical_shift_right, tab("l" + n), ["ia"])
        cp(T.so[:, 0:A], T.ioj[:], ["ioj"], ["so"])
        ts(T.fl[:], T.ia[:], 32.0, ALU.is_ge, ["ia"], ["fl"])
        tt(T.fl[:], T.fl[:], T.slott[:], ALU.mult, ["fl", "slott"], ["fl"])
        tt(T.fl[:], T.fl[:], T.ia[:], ALU.add, ["fl", "ia"], ["fl"])
        cp(T.lu[:], T.fl[:], ["fl"], ["lu"])
        cp(T.so[:, 0:160].indirect(T.lu[:, 0:8]), T.rowc[:], ["rowc", "lu"], ["so"])
        tt(T.dn[:], T.so[:, 0:A], T.mm[:, 0:A], ALU.mult, ["so", "mm"], ["dn"])
        for h in range(2):
            red(T.n2[:, h:h + 1], T.dn[:, 16 * h:16 * h + 16], ["dn"], ["n2%d" % h])
        cp(T["nu" + n][:], T.n2[:], ["n20", "n21"], ["nu" + n])

    def received(t):
        n = str(t)
        xv = T["xr" + n][:, 0:4 * N:4]
        src = ["in_xr" + n, "xrown" + n]
        if t == 0:
            ts(T.ia[:], xv, 6, ALU.logical_shift_right, src, ["ia"], 255, ALU.bitwise_and)
        ts(T.vi[:], xv, 63, ALU.bitwise_and, src, ["vi"])
        if t == 0:
            tt(T.fl[:], T.ia[:], T.fs[:], ALU.mult, ["ia", "fs"], ["fl"])
        tt(T.vm[:], T.vi[:], T.blk[:], ALU.mult, ["vi", "blk"], ["vm"])
        if t == 0:
            tt(T.fl[:], T.fl[:], T.cc[:], ALU.add, ["fl"] + ccs, ["fl"])
        red(T.v[:], T.vm[:], ["vm"], ["v"])
        if t == 0:
            cp(T.lsu[:], T.fl[:], ["fl"], ["lsu"])
            pick("land0", 0, "lx0", 256, T.lsu[:, 0:8], 128, ["in_lx0", "lx0own", "lx0own2", "lsu"], "land0")
        ts(T.zlf[:], T.ibq[:], T.v[:, 0:1], ALU.add, ["ibq", "v"], ["zlf"], 4.0, ALU.mult)
        ts(T.v4[:], T.vi[:], 4.0, ALU.mult, ["vi"], ["v4"])
        cp(T.zl[:], T.zlf[:], ["zlf"], ["zl"])

    def goes(d):
        return slice(CAPP * place(d), CAPP * place(d) + CAPP)

    def serve(t):
        n = str(t)
        land, nt, kp, xq, win = "land" + n, T["nt" + n], "kp" + n, "xq" + n, ("wina", "winb")[t]
        lk = ["land0_c", "land0_s"] if t == 0 else ["in_land1", "land1own_c", "land1own_s"]
        mx(0, 128, land, 0, "kq", 0, lk + ["kq"])
        mx(5, 128, land, 0, "kq", 128, lk + ["kq"])
        for i in range(4):
            mx(1 + i, 128, "h", 128 * i, land, 0, lk + ["h%d" % i], True, False)
        act(T.zs[:, 0:128], bank(0, 128), ["bank0"], ["zs0"])
        cp(T.zs[:, 128:256], bank(5, 128), ["bank5"], ["zs1"])
        tt(T.zg[:], T.zs[:, 0:P].indirect(T.zl[:, 0:4]), T.dm[:], ALU.add, ["zs0", "zs1", "zl", "dm"], ["zg"])
        scan(T.rm[:], T.zg[:], T.zg[:], -2e29, ALU.max, ALU.max, ["zg"], ["rm"])
        for k in range(3):
            ts(T.xb[:, k:4 * N:4], T.bki[:], T.rm[:, 16 * k + 15:16 * k + 16], ALU.add, ["bki", "rm", "xbz"], ["xb%d" % k], T.rm[:, 63:64], ALU.is_lt)
        quant(xq, 0, 128, T.xb[:], ["xbz", "xb0", "xb1", "xb2"], [xq])
        mx(6, 128, "ws", 0, xq, 0, ["ws", xq])
        tt(T.fl[:], bank(6, N), T.v4[:], ALU.add, ["bank6", "v4"], ["fl"])
        cp(T.ct[:], T.fl[:], ["fl"], ["ct"])
        pick(kp, 0, "kq", P, T.ct[:, 0:8], 128, ["kq", "ct"], kp)
        for i in range(4):
            mx(1 + i, 128, "h", 128 * i, kp, 0, [kp + "_c", kp + "_s", "h%d" % i], False, True)
        nodt, rn = T["nodt" + n], T["rn" + n]
        yk = ["yy0", "yy1", "yy2", "yy3"]
        tt(T.yy[:], T.nxf[:, 0:P].indirect(T.ct[:, 0:8]), T.locrow[:], ALU.add, ["nxf", "ct", "locrow"], yk)
        turn(nodt[:], T.yy[:], yk, ["nodt" + n])
        send("rn" + n, lambda d: nodt[:, 32 * (d // 2):32 * (d // 2) + 1], lambda d: rn[:, 4 * rank:4 * rank + 1], ["nodt" + n])
        for i in range(4):
            if i % 2:
                act(nt[:, i:512:4], bank(1 + i, 128), ["bank%d" % (1 + i)], ["nt%s%d" % (n, i)])
            else:
                cp(nt[:, i:512:4], bank(1 + i, 128), ["bank%d" % (1 + i)], ["nt%s%d" % (n, i)])
        quant("new" + n, 0, 128, nt[:], ["nt%s%d" % (n, i) for i in range(4)], ["new" + n])

        def back(d):
            return A + CAPP * seen(d)

        send("ret%s_c" % n, lambda d: codes("new" + n, CAPP * place(d), CAPP * place(d) + CAPP), lambda d: codes(win, back(d), back(d) + CAPP), ["new" + n])
        send("ret%s_s" % n, lambda d: T["new%ss" % n][:, goes(d)], lambda d: T[win + "s"][:, back(d):back(d) + CAPP], ["new" + n])
        cp(rn[:, 4 * rank:4 * rank + 1], nodt[:, 32 * (rank // 2):32 * (rank // 2) + 1], ["nodt" + n], ["rnown" + n])
        pick(win, back(rank), "new" + n, 128, T.ol[:, 0:1], CAPP, ["new" + n, "ol"], win + "own")

    def home(t):
        n = str(t)
        vv = T["vv" + n]
        cp(T.vm[:], T["rn" + n][:, 0:4 * N:4], ["in_rn" + n, "rnown" + n], ["vm"])
        cp(T.mn[:], T.vm[:, 0:N].indirect(T.elst[:, 0:8]), ["vm", "elst"], ["mn"])
        turn(T.win[:, A:160], T.mn[:], ["mn"], ["winr"])
        cp(vv[:], T.win[:, 0:160].indirect(T["nu" + n][:, 0:2]), ["winq", "winr", "nu" + n], ["vv" + n])
        ts(T.dr[:], vv[:], 14, ALU.logical_shift_right, ["vv" + n], ["dr"])

    def number(t):
        n = str(t)
        ts(T.dl[:], T["vv" + n][:], 63, ALU.bitwise_and, ["vv" + n], ["dl"])
        ts(T.dn[:], T.dr[:], 64.0, ALU.mult, ["dr"], ["dn"])
        tt(T["ndf" + n][:], T.dn[:], T.dl[:], ALU.add, ["dl", "dn"], ["ndf" + n])

    for h in range(2):
        ts(T.dr[:, 16 * h:16 * h + 16], T.strb[:, h:A:2], 6, ALU.arith_shift_right, ["strb"], ["dr"])
    for h in range(2):
        ts(T.xm[:, 16 * h:16 * h + 16], T.strb[:, h:A:2], 63, ALU.bitwise_and, ["strb"], ["xm"])
    lists(0)
    for i, c in enumerate(picked):
        k = place(cores.index(c))
        cp(T.pl[:, i:i + 1], T.shx[:, k:k + 1], ["shx"], ["pl%d" % i])
    pick("send0", 0, "qx", 128, T.pl[:, 0:2], 32, ["qx", "pl0", "pl1"], "send0")
    slot = {cores.index(c): i * CAPP for i, c in enumerate(picked)}
    send("pick_c", lambda d: codes("send0", slot[d], slot[d] + CAPP), lambda d: codes("lx0", A * seen(d), A * seen(d) + CAPP), ["send0_c"])
    send("pick_s", lambda d: T.send0s[:, slot[d]:slot[d] + CAPP], lambda d: T.lx0s[:, A * seen(d):A * seen(d) + CAPP], ["send0_s"])
    cp(T.xr0[:, 4 * me:4 * me + 1], T.ti0[:, me:me + 1], tab("l0"), ["xrown0"])
    ts(T.nxh[0:32, :], T.nxt[0:32, :], 6, ALU.arith_shift_right, ["nxt"], ["nxh"])
    ts(T.nxp[0:32, :], T.nxh[0:32, :], float(16384 - 64), ALU.mult, ["nxh"], ["nxp"])
    tt(T.nxp[0:32, :], T.nxp[0:32, :], T.nxt[0:32, :], ALU.add, ["nxp", "nxt"], ["nxp"])
    turn(T.nxq[0:32, :], T.nxp[0:32, :], ["nxp"], ["nxq"])
    dma("s", "nxr", T.nx1[0:1, :], T.nxq[0:16, 0:16], ["nxq"], ["nx1"])
    for k in range(3):
        act(T.wb[:, k:512:4], T.mm[:], ["mm", "wb"], ["wb%d" % k])
    ts(T.pd[:], T.iop[:], 4, ALU.arith_shift_right, ["iop"], ["pd"])
    fill(T.fs[:], 1.0, ["fs"])
    ts(T.cc[:], T.ioj[:, 0:N], 32.0, ALU.mult, ["ioj"], ["cc"])
    tt(T.blk[:], T.pd[:], T.ioj[:, 0:N], ALU.is_equal, ["pd", "ioj"], ["blk"])
    ccs = ["cc"]
    for s, c in enumerate(cores):
        if c != core and core in plans[c][1]:
            k = place(s)
            fill(T.fs[:, k:k + 1], 0.0, ["fs"])
            ts(T.cc[:, k:k + 1], T.r1[:], float(32 * k - 1), ALU.add, ["r1", "cc"], ["cc%d" % k])
            ccs.append("cc%d" % k)
    ts(T.ibq[:], T.ioj[:, 0:4], 0.25, ALU.mult, ["ioj"], ["ibq"])
    quant("kq", 0, P, T.kt[:], ["kt"], ["kq"])
    for i in range(4):
        quant("h", 128 * i, 128 * i + 128, T.hb[:, 3 - i:515 - i], ["hb"], ["h%d" % i])
    ts(T.bki[:], T.blk[:], -1.0, ALU.add, ["blk"], ["bki"], -1e29, ALU.mult)
    ts(T.dm[:], T.mm[:, 0:64], -1.0, ALU.add, ["mm"], ["dm"], 1e29, ALU.mult)
    quant("ws", 0, 128, T.wb[:], ["wb", "wb0", "wb1", "wb2"], ["ws"])
    op("g", lambda e: e.partition_broadcast(T.nxf[:], T.nx1[0:1, :], 128), ["nx1"], ["nxf"])
    iota(T.locrow[:], [[0, 4], [64, 32]], 64 * (A + 32 * (rank // 2)), 0, ["locrow"], True)
    iota(T.el[:], [[2, 4], [0, 2]], 0, 0, ["el"])
    iota(T.rowc[:], [[1, 128]], A, 0, ["rowc"], True)
    iota(T.io16[:], [[16, 8]], -1, 0, ["io16"])
    iota(T.xa1[:], [[16384, A]], 0, 0, ["xa1"], True)
    received(0)
    ts(T.ol[:, 0:1], T.r1[:], float(mine - 1), ALU.add, ["r1"], ["ol"])
    serve(0)
    dma("s", "w", T.wt[:], T.w[:], [], ["wt"])
    dma("s", "ownw", codes("wina", 0, A), codes("qx", 0, A), ["qx"], ["winaq"])
    dma("s", "ownw", T.winas[:, 0:A], T.qxs[:, 0:A], ["qx"], ["winaq2"])
    ts(T.win[:, 0:A], T.dr[:], 16384.0, ALU.mult, ["dr"], ["winq"])
    ts(T.slott[:], T.io16[:], T.r1[:, 0:1], ALU.add, ["io16", "r1"], ["slott"])
    ts(T.ia[:], T.pd[:], 1, ALU.bitwise_and, ["pd"], ["ia"])
    tt(T.win[:, 0:A], T.win[:, 0:A], T.xx[:], ALU.add, ["winq", "xx"], ["winq"])
    ts(T.fl[:], T.ia[:], -1.0 if odd else 1.0, ALU.mult, ["ia"], ["fl"], float(odd), ALU.add)
    tt(T.win[:, 0:A], T.win[:, 0:A], T.xa1[:], ALU.subtract, ["winq", "xa1"], ["winq"])
    tt(T.fl[:], T.fl[:], T.el[:], ALU.add, ["fl", "el"], ["fl"])
    cp(T.elst[:], T.fl[:], ["fl"], ["elst"])
    inverse(0)
    home(0)
    ts(T.xm[:], T.vv0[:], 16383, ALU.bitwise_and, ["vv0"], ["xm"])
    lists(1)
    cp(T.sl[:], T.shx[:], ["shx"], ["sl"])
    wina = ["winaq", "winaq2", "winaown_c", "winaown_s", "in_ret0"]
    pick("send1", 0, "wina", 160, T.sl[:, 0:8], 128, wina + ["sl"], "send1")
    send("land1_c", lambda d: codes("send1", CAPP * place(d), CAPP * place(d) + CAPP),
         lambda d: codes("land1", CAPP * seen(d), CAPP * seen(d) + CAPP), ["send1_c"])
    send("land1_s", lambda d: T.send1s[:, goes(d)], lambda d: T.land1s[:, CAPP * seen(d):CAPP * seen(d) + CAPP], ["send1_s"])
    cp(T.xr1[:, 4 * me:4 * me + 1], T.ti1[:, me:me + 1], tab("l1"), ["xrown1"])
    pick("land1", mine, "send1", 128, T.ol[:, 0:1], CAPP, ["send1_c", "send1_s", "ol"], "land1own")
    for h in range(2):
        cp(T.nd0f[:, 16 * h:16 * h + 16], T.strb[:, h:A:2], ["strb"], ["nd0f"])
    number(0)
    received(1)
    serve(1)
    dma("s", "nd0", T.nd[0:1, :], T.nd0f[0:1, :], ["nd0f"], [])
    dma("s", "nd1", T.nd[1:2, :], T.ndf0[0:1, :], ["ndf0"], [])
    cp(T.win[:, 0:A], T.vv0[:], ["vv0"], ["winq"])
    inverse(1)
    pick("winb", 0, "wina", 160, T.nu0[:, 0:2], A, wina + ["nu0"], "winbq")
    quant("wq", 0, 128, T.wt[:], ["wt"], ["wq"])
    quant("fin", 0, 128, T.xt[:], ["xt", "xtz"], ["fin_c", "fin_s"])
    home(1)
    number(1)
    dma("s", "nd2", T.nd[2:3, :], T.ndf1[0:1, :], ["ndf1"], [])
    pick("fin", 0, "winb", 160, T.nu1[:, 0:2], A, ["winbq_c", "winbq_s", "winbown_c", "winbown_s", "in_ret1", "nu1"], "fin")
    mx(7, 128, "wq", 0, "fin", 0, ["wq", "fin_c", "fin_s"])
    act(T.ys[:], bank(7, A), ["bank7"], ["ys"])
    dma("a", "y", T.y[:], T.ys[:], ["ys"], [])
    dma("s", "oc", T.oc[:], codes("fin", 0, A), ["fin_c"], [])
    for k in range(4):
        dma("s" if k % 2 else "a", "osc", T.osc[4 * k:4 * k + 4, :], T.fins[32 * k:32 * k + 4, 0:A], ["fin_s"], [])
    g.wait_ge(T.sem.left, left[0])
    for q, s in sems.items():
        g.wait_ge(T.sem[s], count[q])
    for s, v in dcount.items():
        g.wait_ge(T.sem[s], v)
